import numpy as np, ml_dtypes
CORES = [16,18,20,22]
N = 4
import mx_ref
BF = ml_dtypes.bfloat16
def entries(a):
    return np.ascontiguousarray(a.T).reshape(-1)
def table(e):
    return np.ascontiguousarray(np.reshape(e, (-1, 16)).T).astype(np.int32)
def pick(q, e):
    c = np.concatenate([q[0].reshape(128, -1, 4), np.zeros((128, 1, 4), np.uint8)], axis=1); s = np.concatenate([q[1], np.ones((16, 1), np.uint8)], axis=1)
    return (np.ascontiguousarray(c[:, e].reshape(128, -1)), np.ascontiguousarray(s[:, e]))
def join(*qs):
    return (np.concatenate([q[0] for q in qs], axis=1), np.concatenate([q[1] for q in qs], axis=1))
def put(q, e, v):
    c, s = q[0].reshape(128, -1, 4).copy(), q[1].copy(); c[:, e] = v[0].reshape(128, -1, 4); s[:, e] = v[1]
    return (c.reshape(128, -1), s)
def pk(c, s):
    return (np.ascontiguousarray(c), mx_ref.live(s))
def emit(q):
    return q[0], q[1]
def packed(v, rng):
    q = [mx_ref.quantize(np.ascontiguousarray(v[r])) for r in range(N)]
    return np.stack([a for a, b in q]), np.stack([mx_ref.plane(b, rng) for a, b in q])
def decode(q):
    o = []
    for b in range(4):
        e = np.zeros((128, 128, 4), np.float32); e[np.arange(128), np.arange(128), b] = 1
        o.append(mx_ref.matmul(mx_ref.quantize(e.reshape(128, 512).astype(BF)), q))
    return np.stack(o, axis=2).reshape(128, -1)
def f(rng, *shape):
    return mx_ref.flush((rng.standard_normal(shape, dtype=np.float32) * np.exp2(rng.integers(-2, 3, shape[:-1] + (1,)))).astype(BF))
def wide(rng, *shape, cols=0):
    v = rng.standard_normal(shape, dtype=np.float32) * np.exp2(rng.integers(-12, 13, shape)).astype(np.float32)
    if cols: v *= np.repeat(np.exp2(rng.integers(-cols, cols + 1, shape[:-2] + (1, shape[-1] // 4))) * (rng.random(shape[:-2] + (1, shape[-1] // 4)) > 0.0625), 4, axis=-1).astype(np.float32)
    return mx_ref.flush(v.astype(BF))
C, S, CAPP = 1024, 512, 160
def big(v, k):
    v = v.astype(np.float32) * np.float32(k)
    v[np.abs(v) < np.float32(2.0 ** -16)] = 0
    return v.astype(BF)
def names(rng, n, each):
    out, at, m = [None] * N, 0, int(n.sum())
    if not each:
        left = np.full(C, 2)
        for s in rng.permutation(N):
            out[s] = rng.permutation(np.flatnonzero(left))[:n[s]]; left[out[s]] -= 1
        return out
    a = rng.permutation(C)[:m // each]
    if each == 2: a = np.concatenate([a, rng.permutation(a)])
    for s in rng.permutation(N):
        out[s] = a[at:at + n[s]]; at += n[s]
    return out
def lists(rng, each=0, full=False, gaps=False, silent=False):
    sn, tc = np.full((N, N * CAPP), -1), np.full((N, N * CAPP), -1)
    n = np.full((N, N), CAPP) if full else rng.integers(CAPP // 4, CAPP, (N, N))
    if gaps: n[:] = CAPP - CAPP // 6
    if silent: n[:, int(rng.integers(0, N))] = 0
    for q in range(N):
        t = names(rng, n[:, q], each)
        for s in range(N): tc[q, s * CAPP + rng.permutation(CAPP)[:n[s, q]]] = t[s]
    for s in range(N):
        used = np.concatenate([tc[q, s * CAPP:s * CAPP + CAPP] >= 0 for q in range(N)])
        e = np.concatenate([rng.permutation(S), rng.integers(0, S, N * CAPP)])[:used.sum()]
        sn[s, used] = rng.permutation(e)
    return {"sn": np.stack([table(v) for v in sn]), "tc": np.stack([table(v) for v in tc])}
def setup_inputs(rng):
    c, p = packed(big(f(rng, N, 128, 4 * C), 1), rng)
    return {"wc": c, "ws": p, "gr": big(f(rng, N, 128, 4 * S), 8), **lists(rng)}
def setup_inputs_cancel(rng):
    tc, P = lists(rng, each=2, full=True, gaps=True)["tc"], S // 2
    x = rng.integers(4, 8, (128, P, 4)) * np.exp2(rng.integers(-2, 1, (128, P, 4))) * rng.choice([-1.0, 1.0], (128, P, 4)) * np.exp2(rng.integers(-2, 3, (128, P, 1)))
    h = rng.integers(0, P, (N, C))
    c, p = packed(np.stack([x[:, h[q]].reshape(128, -1) for q in range(N)]).astype(np.float32).astype(BF), rng)
    g, sn = np.zeros((N, 128, S, 4), np.float32), np.full((N, N * CAPP), -1)
    at = np.stack([rng.permutation(S) for s in range(N)])
    for s in range(N):
        g[s][:, at[s, :P]] = 8 * x
        g[s][:, at[s, P:]] = 8 * x * np.exp2(-rng.integers(21, 25, (P, 1)))
    for q in range(N):
        t = entries(tc[q]).reshape(N, CAPP)
        o = rng.permutation(np.unique(t[t >= 0]))
        late, seen = np.zeros(C, bool), np.zeros(C, bool)
        late[o[:o.size // 2]] = True
        for s in range(N):
            k = np.flatnonzero(t[s] >= 0); e = t[s][k]
            small = seen[e] != late[e]
            sn[s, q * CAPP + k] = at[s][P * small + h[q, e]]
            seen[e] = True
    return {"wc": c, "ws": p, "gr": g.reshape(N, 128, 4 * S).astype(BF), "sn": np.stack([table(v) for v in sn]), "tc": tc}
def setup_inputs_full(rng):
    return {**setup_inputs(rng), **lists(rng, full=True)}
def setup_inputs_most(rng):
    return {**setup_inputs(rng), **lists(rng, each=1, full=True, silent=True)}
def setup_inputs_spread(rng):
    d = setup_inputs(rng)
    d["wc"], d["ws"] = packed(big(wide(rng, N, 128, 4 * C, cols=8), 1), rng)
    d["gr"] = big(wide(rng, N, 128, 4 * S, cols=8), 8)
    return d
def setup_inputs_twice(rng):
    return {**setup_inputs(rng), **lists(rng, each=2, full=True)}
def check_inputs(d):
    b = []
    for r in range(N):
        a, t = entries(d["sn"][r]), entries(d["tc"][r])
        if a.min() < -1 or a.max() >= S: b.append("sn")
        sent = np.concatenate([entries(d["sn"][s])[r * CAPP:r * CAPP + CAPP] for s in range(N)])
        bad = t.min() < -1 or t.max() >= C or ((t >= 0) != (sent >= 0)).any()
        for s in range(N):
            v = t[s * CAPP:s * CAPP + CAPP]; v = v[v >= 0]
            bad = bad or len(set(v.tolist())) != v.size
        if bad or (np.unique(t[t >= 0], return_counts=True)[1] > 2).any(): b.append("tc")
    return b
def reference(wc, ws, gr, sn, tc):
    oc, osc, up = np.zeros((N, 128, 4 * C), np.uint8), np.zeros((N, 16, C), np.uint8), np.zeros((N, 1, C), np.float32)
    g = [decode(mx_ref.quantize(np.ascontiguousarray(gr[s]))).reshape(128, S, 4) for s in range(N)]
    for q in range(N):
        w = pk(wc[q], ws[q])
        v = decode(w).reshape(128, C, 4)
        for s in range(N):
            e, t = entries(sn[s])[q * CAPP:q * CAPP + CAPP], entries(tc[q])[s * CAPP:s * CAPP + CAPP]
            k = t >= 0
            v[:, t[k]] = v[:, t[k]] - g[s][:, e[k]] * np.float32(0.125)
            up[q, 0, t[k]] += 1
        named = np.flatnonzero(up[q, 0])
        new = mx_ref.quantize(np.ascontiguousarray(v.reshape(128, -1).astype(BF)))
        oc[q], osc[q] = emit(put(w, named, pick(new, named)))
    return {"oc": oc, "osc": osc, "up": up}

@@ -1,0 +1,321 @@
+from concourse.bass import DstId, RemoteDMATransfer
+from concourse.mybir import dt, AluOpType, ActivationFunctionType
+
+C, S, CAP, N = 1024, 512, 160, 4
+K = N * CAP
+H0 = 3 * CAP
+M = 74
+WIN = 16 * M
+NONE = 2000.0
+X4 = "float8_e4m3fn_x4"
+
+
+def _sb(dtype, **widths):
+    return {name: ("sbuf", [128, n], dtype) for name, n in widths.items()}
+
+
+SCRATCH = {
+    **_sb("bfloat16", ones=516, dg=516, dm=516, zt=512, grt=4 * S, nw=4 * K),
+    **_sb(X4, ec=512, mc=512, gq=S, snd=H0, land=K + 128, wsrc=C, wi=K, par=H0, tab=K + C, fin=C),
+    **_sb("uint8", es=512, ms=512, gqs=S, snds=H0, lands=K + 128, wsrcs=C, wis=K, pars=H0, tabs=K + C, fins=C),
+    **_sb("int32", pi=1, p15=1, p96=1, kb=40, kk=40, fq=30, snl=40, tcl=40, la=40, lb=40, ln=40, la2=40, ln2=40, ls=40, lp=40),
+    **_sb("float32", icol=1, ic74=1, pcol=1, jj=CAP, vals=CAP, b16=64, jw=64, ff=30, fa=30, fb=30, fc=30, win=WIN, rn=H0, rp=H0,
+          rw=90, fw=4 * M, f1=2 * M, f2=64, f3=64, c1=4 * M, c2=2 * M, c3=64, c4=64),
+    **_sb("uint16", pmo=30, sno=40, wo=40, lto=10, poso=30, paro=30, fino=64),
+    "ps": ("psum", [128, 4096], "float32"),
+}
+SEMAPHORES = ["v", "s", "t", "p", "ltc", "lsn", "lgr0", "lgr1", "lw", "ltab", "xf", "xr", "stored", "arr", "loc"]
+
+
+def code_engines(src, dst, cores, topo):
+    e = topo.engines(src, dst)
+    even, odd = e[0::2], e[1::2]
+    if topo.die(src) == topo.die(dst):
+        return odd
+    far = [c for c in cores if topo.die(c) != topo.die(src)]
+    h = len(even) // 2
+    return even[:h] if far.index(dst) == 0 else even[h:]
+
+
+def scale_engines(src, dst, cores, topo):
+    e = topo.engines(src, dst)
+    even, odd = e[0::2], e[1::2]
+    if topo.die(src) == topo.die(dst):
+        return even[:len(even) // 2]
+    far = [c for c in cores if topo.die(c) != topo.die(src)]
+    h = len(odd) // 2
+    return odd[:h] if far.index(dst) == 0 else odd[h:]
+
+
+def bits(e):
+    m = 0
+    for k in e:
+        m |= 1 << k
+    return m
+
+
+def rank_program(g, core, T, topo):
+    rank = T.rank_of(core)
+    if rank is None:
+        return
+    cores = list(T.cores)
+    A = AluOpType
+    COPY = ActivationFunctionType.Copy
+    v, sc, te, sy = g.vector, g.scalar, g.tensor, g.sync
+    queue = {"g": g, "v": v, "s": sc, "t": te, "y": sy}
+    count = {"v": 0, "s": 0, "t": 0, "p": 0, "stored": 0}
+    seen = {}
+
+    def wait(q, sem, val):
+        if seen.get((q, sem), 0) < val:
+            queue[q].wait_ge(T.sem[sem], val)
+            seen[(q, sem)] = val
+
+    def done(sem, ins):
+        ins.then_inc(T.sem[sem], 1)
+        count[sem] += 1
+        return count[sem]
+
+    def V(ins):
+        return done("v", ins)
+
+    def Sc(ins):
+        return done("s", ins)
+
+    def P(ins):
+        return done("p", ins)
+
+    def u8(ap):
+        return ap.bitcast(dt.uint8)
+
+    def u32(ap):
+        return ap.bitcast(dt.uint32)
+
+    for q, lo in ((sy, 0), (sc, 4)):
+        for u in range(lo, lo + 4):
+            q.dma_start(T.tcl[16 * u:16 * u + 16, :], T.tc[:, :]).then_inc(T.sem.ltc, 16)
+        h = lo // 4
+        q.dma_start(T.grt[:, 1024 * h:1024 * h + 1024], T.gr[:, 1024 * h:1024 * h + 1024]).then_inc(T.sem["lgr%d" % h], 16)
+        for u in range(lo, lo + 4):
+            q.dma_start(T.snl[16 * u:16 * u + 16, :], T.sn[:, :]).then_inc(T.sem.lsn, 16)
+    sy.dma_start(u8(T.wsrc[:, :]), T.wc[:, :]).then_inc(T.sem.lw, 16)
+    sc.dma_start(T.wsrcs[:, :], T.ws[:, :]).then_inc(T.sem.lw, 16)
+
+    v_ones = V(v.memset(T.ones[:, :], 1.0))
+    p_pi = P(g.iota(T.pi[:, :], [[0, 1]], 0, 1))
+    P(g.iota(T.kb[:, :], [[0, 4], [1, 10]], 64 - (15 * M - 1), 0))
+    P(g.iota(T.jj[:, :], [[1, CAP]], 0, 0, allow_small_or_imprecise_dtypes=True))
+    p_b16 = P(g.iota(T.b16[:, :], [[16, 64]], 0, 0, allow_small_or_imprecise_dtypes=True))
+    wait("g", "v", v_ones)
+    p_dg = P(g.affine_select(T.dg[:, :], T.ones[:, :], [[1, 516]], A.is_equal, 0.0, -3, -4))
+
+    V(v.memset(T.win[:, :], NONE))
+    V(v.memset(T.zt[:, :], 0.0))
+    wait("v", "p", p_pi)
+    V(v.tensor_scalar(T.p15[:, :], T.pi[:, :], 15, None, A.bitwise_and))
+    x = V(v.tensor_scalar(T.p96[:, :], T.pi[:, :], 96, None, A.bitwise_and))
+    wait("v", "v", x)
+    V(v.tensor_copy(T.icol[:, :], T.p15[:, :]))
+    V(v.tensor_scalar(T.ic74[:, :], T.p15[:, :], float(M), None, A.mult))
+    x = V(v.tensor_scalar(T.pcol[:, :], T.p96[:, :], 5.0, None, A.mult))
+    wait("v", "v", x)
+    wait("v", "p", p_b16)
+    V(v.tensor_scalar(T.kk[:, :], T.kb[:, :], T.ic74[:, 0:1], None, A.add))
+    V(v.tensor_scalar(T.vals[:, :], T.jj[:, :], T.pcol[:, 0:1], None, A.add))
+    V(v.tensor_scalar(T.jw[:, :], T.b16[:, :], T.icol[:, 0:1], float(K), A.add, A.add))
+    x = V(v.tensor_scalar(T.ff[:, :], T.b16[:, 0:30], T.icol[:, 0:1], None, A.add))
+    wait("v", "v", x)
+    V(v.tensor_scalar(T.fq[:, :], T.ff[:, :], 1.0 / 30.0, -29.0 / 60.0, A.mult, A.add))
+    x = V(v.tensor_scalar(T.fb[:, :], T.ff[:, :], 16.0, None, A.mult))
+    wait("v", "v", x)
+    x = V(v.tensor_scalar(T.fa[:, :], T.fq[:, :], -479.0, None, A.mult))
+    wait("v", "v", x)
+    x = V(v.tensor_tensor(T.fc[:, :], T.fa[:, :], T.fb[:, :], A.add))
+    wait("v", "v", x)
+    V(v.tensor_copy(T.pmo[:, :], T.fc[:, :]))
+    V(v.quantize_mx(T.land[:, K:K + 128], T.lands[:, K:K + 128], T.zt[:, :]))
+
+    wait("v", "ltc", 128)
+    V(v.tensor_scalar(T.la[:, :], T.tcl[:, :], 15, None, A.bitwise_and))
+    V(v.tensor_scalar(T.lb[:, :], T.tcl[:, :], 4, None, A.arith_shift_right))
+    x = V(v.tensor_scalar(T.ln[:, :], T.tcl[:, :], 0.0, None, A.is_lt))
+    wait("v", "v", x)
+    V(v.tensor_scalar(T.la2[:, :], T.la[:, :], float(M), None, A.mult))
+    x = V(v.tensor_tensor(T.ln2[:, :], T.ln[:, :], T.kk[:, :], A.mult))
+    wait("v", "v", x)
+    x = V(v.tensor_tensor(T.ls[:, :], T.la2[:, :], T.lb[:, :], A.add))
+    wait("v", "v", x)
+    x = V(v.tensor_tensor(T.lp[:, :], T.ls[:, :], T.ln2[:, :], A.add))
+    wait("v", "v", x)
+    for t in range(N):
+        x = V(v.tensor_copy(T.lto[32 * t:32 * t + 32, :], T.lp[32 * t:32 * t + 32, 10 * t:10 * t + 10]))
+    wait("v", "v", x)
+    v_scat = V(v.tensor_copy(T.win[:, :].indirect(T.lto[:, :]), T.vals[:, :]))
+    V(v.tensor_copy(T.poso[:, :], T.lp[:, 0:30]))
+    v_wo = V(v.tensor_copy(T.wo[:, :], T.tcl[:, :]))
+    wait("v", "lsn", 128)
+    V(v.tensor_copy(T.sno[:, :], T.snl[:, :]))
+
+    for h in range(2):
+        wait("v", "lgr%d" % h, 16)
+        v_gq = V(v.quantize_mx(T.gq[:, 256 * h:256 * h + 256], T.gqs[:, 256 * h:256 * h + 256], T.grt[:, 1024 * h:1024 * h + 1024]))
+    wait("v", "v", v_gq)
+    wait("s", "v", v_gq)
+    runs = [(a, b) for a, b in ((0, 10 * rank), (10 * rank + 10, 40)) if b > a]
+    at = 0
+    for a, b in runs:
+        n = 16 * (b - a)
+        v_snd = V(v.tensor_copy(u32(T.snd[:, at:at + n]), u32(T.gq[:, :]).indirect(T.sno[:, a:b])))
+        s_snd = Sc(sc.activation(T.snds[:, at:at + n], T.gqs[:, :].indirect(T.sno[:, a:b]), COPY))
+        at += n
+    own = slice(CAP * rank, CAP * rank + CAP)
+    V(v.tensor_copy(u32(T.land[:, own]), u32(T.gq[:, :]).indirect(T.sno[:, 10 * rank:10 * rank + 10])))
+    s_own = Sc(sc.activation(T.lands[:, own], T.gqs[:, :].indirect(T.sno[:, 10 * rank:10 * rank + 10]), COPY))
+
+    others = [q for q in range(N) if q != rank]
+    sent = 0
+    for buf, dst, engines, q, need in (("snd", "land", code_engines, "v", v_snd), ("snds", "lands", scale_engines, "s", s_snd)):
+        transfers = []
+        for k, o in enumerate(others):
+            rid, pid, _ = topo.addr(cores[o])
+            e = engines(core, cores[o], cores, topo)
+            src, to = T[buf][:, CAP * k:CAP * k + CAP], T[dst][:, own]
+            if buf == "snd":
+                src, to = u8(src), u8(to)
+            transfers.append(RemoteDMATransfer(dst_ids=[DstId(rid=rid, pnc=pid)], dma_engine_mask=bits(e), remote_sem=T.sem.arr, src=src, dst=to))
+            sent += len(e)
+        wait("g", q, need)
+        g.remote_dma_fused(transfers, local_sem=T.sem.loc)
+    arrive = sum(len(f(cores[o], core, cores, topo)) for o in others for f in (code_engines, scale_engines))
+
+    wait("v", "p", p_dg)
+    V(v.tensor_scalar(T.dm[:, :], T.dg[:, :], -0.125, None, A.mult))
+    for b in range(4):
+        x = V(v.quantize_mx(T.ec[:, 128 * b:128 * b + 128], T.es[:, 128 * b:128 * b + 128], T.dg[:, 3 - b:515 - b]))
+    wait("v", "lw", 32)
+    wait("s", "lw", 32)
+    wait("s", "v", v_wo)
+    v_wi = V(v.tensor_copy(u32(T.wi[:, :]), u32(T.wsrc[:, :]).indirect(T.wo[:, :])))
+    s_wi = Sc(sc.activation(T.wis[:, :], T.wsrcs[:, :].indirect(T.wo[:, :]), COPY))
+    wait("v", "v", x)
+    for b in range(4):
+        v_m = V(v.quantize_mx(T.mc[:, 128 * b:128 * b + 128], T.ms[:, 128 * b:128 * b + 128], T.dm[:, 3 - b:515 - b]))
+
+    def product(const, b, half, mov, movs, first, last):
+        c, s_ = (T.ec, T.es) if const == "e" else (T.mc, T.ms)
+        n = H0 if half == 0 else CAP
+        bank = 512 * (4 * half + b)
+        return te.matmul_mx(T.ps[:, bank:bank + n], c[:, 128 * b:128 * b + 128], s_[:, 128 * b:128 * b + 128], mov, movs, first, last)
+
+    wait("t", "v", v_wi)
+    wait("t", "s", s_wi)
+    for b in range(4):
+        product("e", b, 0, T.wi[:, 0:H0], T.wis[:, 0:H0], True, False)
+    for b in range(4):
+        product("e", b, 1, T.wi[:, H0:K], T.wis[:, H0:K], True, False)
+
+    x = Sc(sc.activation(T.rn[:, :], T.win[:, :].indirect(T.poso[:, :]), COPY))
+    wait("s", "s", x)
+    s_rp = Sc(sc.activation(T.rp[:, :], T.rn[:, :].indirect(T.pmo[:, :]), COPY))
+
+    wait("y", "v", v_scat)
+    for t in range(N):
+        sy.dma_start(T.fw[:, M * t:M * t + M], T.win[32 * t:32 * t + 8, :]).then_inc(T.sem.xf, 16)
+    wait("y", "s", s_rp)
+    for k, t in enumerate((3, 2, 1)):
+        sy.dma_start(T.rw[:, 30 * k:30 * k + 30], T.rp[32 * t:32 * t + 8, :]).then_inc(T.sem.xr, 16)
+    sy.dma_start(u8(T.tab[:, K:K + C]), T.wc[:, :]).then_inc(T.sem.ltab, 16)
+    sy.dma_start(T.tabs[:, K:K + C], T.ws[:, :]).then_inc(T.sem.ltab, 16)
+
+    wait("v", "xf", 64)
+    x = V(v.tensor_tensor(T.f1[:, :], T.fw[:, 0:2 * M], T.fw[:, 2 * M:4 * M], A.min))
+    wait("v", "v", x)
+    x = V(v.tensor_tensor(T.f2[:, :], T.f1[:, 0:64], T.f1[:, M:M + 64], A.min))
+    wait("v", "v", x)
+    x = V(v.tensor_tensor(T.f3[:, :], T.f2[:, :], T.jw[:, :], A.min))
+    wait("v", "v", x)
+    V(v.tensor_copy(T.fino[:, :], T.f3[:, :]))
+    wait("v", "xr", 48)
+    x = V(v.tensor_tensor(T.rw[:, 0:20], T.rw[:, 0:20], T.rw[:, 30:50], A.min))
+    wait("v", "v", x)
+    x = V(v.tensor_tensor(T.rw[:, 0:10], T.rw[:, 0:10], T.rw[:, 60:70], A.min))
+    wait("v", "v", x)
+    v_paro = V(v.tensor_scalar(T.paro[:, :], T.rw[:, 0:30], float(K), None, A.min))
+
+    wait("v", "arr", arrive)
+    wait("s", "arr", arrive)
+    wait("t", "arr", arrive)
+    wait("v", "v", v_paro)
+    wait("s", "v", v_paro)
+    wait("s", "s", s_own)
+    v_par = V(v.tensor_copy(u32(T.par[:, :]), u32(T.land[:, :]).indirect(T.paro[:, :])))
+    s_par = Sc(sc.activation(T.pars[:, :], T.lands[:, :].indirect(T.paro[:, :]), COPY))
+
+    wait("t", "v", v_m)
+    wait("t", "s", s_own)
+    for b in range(4):
+        product("m", b, 0, T.land[:, 0:H0], T.lands[:, 0:H0], False, False)
+    wait("t", "v", v_par)
+    wait("t", "s", s_par)
+    t_done = {}
+    for b in range(4):
+        t_done[(b, 0)] = done("t", product("m", b, 0, T.par[:, :], T.pars[:, :], False, True))
+    for b in range(4):
+        t_done[(b, 1)] = done("t", product("m", b, 1, T.land[:, H0:K], T.lands[:, H0:K], False, True))
+
+    x = V(v.tensor_scalar(T.c1[0:32, :], T.fw[0:32, :], float(K), None, A.is_lt))
+    wait("v", "v", x)
+    x = V(v.tensor_tensor(T.c2[0:32, :], T.c1[0:32, 0:2 * M], T.c1[0:32, 2 * M:4 * M], A.add))
+    wait("v", "v", x)
+    x = V(v.tensor_tensor(T.c3[0:32, :], T.c2[0:32, 0:64], T.c2[0:32, M:M + 64], A.add))
+    wait("v", "v", x)
+    v_up = V(v.transpose(T.c4[0:32, :], T.c3[0:32, :]))
+    wait("y", "v", v_up)
+    for b in range(2):
+        sy.dma_start(T.up[0:1, 512 * b:512 * b + 512], T.c4[0:32, 32 * b:32 * b + 16]).then_inc(T.sem.stored, 16)
+        count["stored"] += 16
+
+    last = {}
+
+    def cast(q, b, half):
+        lo, n = (0, H0) if half == 0 else (H0, CAP)
+        wait(q, "t", t_done[(b, half)])
+        bank = 512 * (4 * half + b)
+        out, src = T.nw[:, 4 * lo + b:4 * (lo + n):4], T.ps[:, bank:bank + n]
+        if q == "v":
+            last["v"] = V(v.tensor_copy(out, src))
+        else:
+            last["s"] = Sc(sc.activation(out, src, COPY))
+
+    cast("s", 0, 0)
+    cast("v", 1, 0)
+    cast("s", 2, 0)
+    cast("v", 3, 0)
+    wait("v", "v", last["v"])
+    wait("v", "s", last["s"])
+    V(v.quantize_mx(T.tab[:, 0:H0], T.tabs[:, 0:H0], T.nw[:, 0:4 * H0]))
+    for b in range(4):
+        cast("s", b, 1)
+    wait("v", "s", last["s"])
+    v_new = V(v.quantize_mx(T.tab[:, H0:K], T.tabs[:, H0:K], T.nw[:, 4 * H0:4 * K]))
+
+    wait("v", "ltab", 32)
+    wait("s", "ltab", 32)
+    wait("v", "v", v_new)
+    wait("s", "v", v_new)
+    for h in range(2):
+        lst = T.fino[:, 32 * h:32 * h + 32]
+        x = V(v.tensor_copy(u32(T.fin[:, 512 * h:512 * h + 512]), u32(T.tab[:, :]).indirect(lst)))
+        s_fin = Sc(sc.activation(T.fins[:, 512 * h:512 * h + 512], T.tabs[:, :].indirect(lst), COPY))
+        wait("y", "v", x)
+        sy.dma_start(T.oc[:, 2048 * h:2048 * h + 2048], u8(T.fin[:, 512 * h:512 * h + 512])).then_inc(T.sem.stored, 16)
+        count["stored"] += 16
+    wait("s", "s", s_fin)
+    for k in range(4):
+        sc.dma_start(T.osc[4 * k:4 * k + 4, :], T.fins[32 * k:32 * k + 4, :]).then_inc(T.sem.stored, 16)
+        count["stored"] += 16
+    wait("y", "stored", count["stored"])
+
+    wait("g", "loc", sent)
+    for sem in ("v", "s", "t", "p"):
+        wait("g", sem, count[sem])

@@ -4,9 +4,11 @@ from concourse.mybir import dt, AluOpType, ActivationFunctionType
 C, S, CAP, N = 1024, 512, 160, 4
 K = N * CAP
 H0 = 3 * CAP
-M = 74
-WIN = 16 * M
-NONE = 2000.0
+M = C // 16
+WIN = C + CAP
+STEP = 2048
+HELD = 4 * STEP
+NONE = 2.0 * HELD
 X4 = "float8_e4m3fn_x4"
 
 
@@ -15,16 +17,25 @@ def _sb(dtype, **widths):
 
 
 SCRATCH = {
-    **_sb("bfloat16", ones=516, dg=516, dm=516, zt=512, grt=4 * S, nw=4 * K),
+    **_sb("bfloat16", ones=296, eye=128, dg=516, dm=516, zt=512, grt=4 * S, nw=4 * K),
     **_sb(X4, ec=512, mc=512, gq=S, snd=H0, land=K + 128, wsrc=C, wi=K, par=H0, tab=K + C, fin=C),
     **_sb("uint8", es=512, ms=512, gqs=S, snds=H0, lands=K + 128, wsrcs=C, wis=K, pars=H0, tabs=K + C, fins=C),
-    **_sb("int32", pi=1, p15=1, p96=1, kb=40, kk=40, fq=30, snl=40, tcl=40, la=40, lb=40, ln=40, la2=40, ln2=40, ls=40, lp=40),
-    **_sb("float32", icol=1, ic74=1, pcol=1, jj=CAP, vals=CAP, b16=64, jw=64, ff=30, fa=30, fb=30, fc=30, win=WIN, rn=H0, rp=H0,
-          rw=90, fw=4 * M, f1=2 * M, f2=64, f3=64, c1=4 * M, c2=2 * M, c3=64, c4=64),
-    **_sb("uint16", pmo=30, sno=40, wo=40, lto=10, poso=30, paro=30, fino=64),
+    **_sb("int32", pi=1, p15=1, p96=1, kb=40, kk=40, tcl=72, tcr=72, la=72, lb=72, la2=72, ls=72, ln=40, ln2=40, lp=40,
+          xl=32, snl=40, f3=64, f4=64),
+    **_sb("float32", icol=1, jcol=1, pcol=1, ncol=1, jj=CAP, vals=CAP, b16=64, jw=64, win=WIN, rn=512, rw=96,
+          fw=4 * M, f1=2 * M, f2=64, c1=4 * M, c2=2 * M, c3=64, c4=64),
+    **_sb("uint16", sno=40, wo=40, lto=10, poso=32, paro=30, fino=64),
     "ps": ("psum", [128, 4096], "float32"),
 }
-SEMAPHORES = ["v", "s", "t", "p", "ltc", "lsn", "lgr0", "lgr1", "lw", "ltab", "xf", "xr", "stored", "arr", "loc"]
+SEMAPHORES = ["v", "s", "t", "p", "ltc", "lx", "lsn", "lgr0", "lgr1", "lw", "ltab", "xf", "xr", "stored", "arr", "loc", "go"]
+
+
+def partners(rank):
+    return [s for s in range(3) if s != rank] + [rank] if rank != 3 else [0, 1, 2]
+
+
+def items(rank):
+    return [s for s in range(N) if s != rank] + [rank]
 
 
 def code_engines(src, dst, cores, topo):
@@ -60,11 +71,12 @@ def rank_program(g, core, T, topo):
         return
     cores = list(T.cores)
     A = AluOpType
-    COPY = ActivationFunctionType.Copy
+    COPY, ID = ActivationFunctionType.Copy, ActivationFunctionType.Identity
     v, sc, te, sy = g.vector, g.scalar, g.tensor, g.sync
     queue = {"g": g, "v": v, "s": sc, "t": te, "y": sy}
     count = {"v": 0, "s": 0, "t": 0, "p": 0, "stored": 0}
     seen = {}
+    order, par = items(rank), partners(rank)
 
     def wait(q, sem, val):
         if seen.get((q, sem), 0) < val:
@@ -91,86 +103,97 @@ def rank_program(g, core, T, topo):
     def u32(ap):
         return ap.bitcast(dt.uint32)
 
+    def runs(where):
+        k, r = 0, []
+        while k < len(where):
+            n = 1
+            while k + n < len(where) and where[k + n] == where[k] + n:
+                n += 1
+            r.append((10 * k, 10 * where[k], 10 * n))
+            k += n
+        return r
+
+    v_xl = V(v.memset(T.xl[:, :], 0))
+    v_ones = V(v.memset(T.ones[:, :], 1.0))
     for q, lo in ((sy, 0), (sc, 4)):
         for u in range(lo, lo + 4):
-            q.dma_start(T.tcl[16 * u:16 * u + 16, :], T.tc[:, :]).then_inc(T.sem.ltc, 16)
-        h = lo // 4
+            q.dma_start(T.tcl[16 * u:16 * u + 16, 32:72], T.tc[:, :]).then_inc(T.sem.ltc, 16)
+    wait("y", "v", v_xl)
+    for t in (1, 2, 3):
+        sy.dma_start(T.xl[32 * t:32 * t + 32, 0:16], T.tc[:, 0:32]).then_inc(T.sem.lx, 16)
+    for h, q in ((0, sc), (1, sy)):
         q.dma_start(T.grt[:, 1024 * h:1024 * h + 1024], T.gr[:, 1024 * h:1024 * h + 1024]).then_inc(T.sem["lgr%d" % h], 16)
-        for u in range(lo, lo + 4):
+        for u in range(4 * h, 4 * h + 4):
             q.dma_start(T.snl[16 * u:16 * u + 16, :], T.sn[:, :]).then_inc(T.sem.lsn, 16)
     sy.dma_start(u8(T.wsrc[:, :]), T.wc[:, :]).then_inc(T.sem.lw, 16)
     sc.dma_start(T.wsrcs[:, :], T.ws[:, :]).then_inc(T.sem.lw, 16)
 
-    v_ones = V(v.memset(T.ones[:, :], 1.0))
     p_pi = P(g.iota(T.pi[:, :], [[0, 1]], 0, 1))
-    P(g.iota(T.kb[:, :], [[0, 4], [1, 10]], 64 - (15 * M - 1), 0))
+    wait("g", "v", v_ones)
+    p_eye = P(g.affine_select(T.eye[:, :], T.ones[:, 0:128], [[-1, 128]], A.is_equal, 0.0, 0, 1))
+    p_kb = P(g.iota(T.kb[:, :], [[0, 4], [16, 10]], C - (15 * M - 1), 0))
     P(g.iota(T.jj[:, :], [[1, CAP]], 0, 0, allow_small_or_imprecise_dtypes=True))
     p_b16 = P(g.iota(T.b16[:, :], [[16, 64]], 0, 0, allow_small_or_imprecise_dtypes=True))
-    wait("g", "v", v_ones)
-    p_dg = P(g.affine_select(T.dg[:, :], T.ones[:, :], [[1, 516]], A.is_equal, 0.0, -3, -4))
+    wait("s", "v", v_ones)
+    for h in range(2):
+        s_dm = Sc(sc.activation(T.dm[:, 258 * h:258 * h + 258], T.ones[:, 0:258], COPY, scale=0.0))
+    for h in range(4):
+        Sc(sc.activation(T.win[:, 296 * h:296 * h + 296], T.ones[:, :], COPY, scale=NONE))
 
-    V(v.memset(T.win[:, :], NONE))
-    V(v.memset(T.zt[:, :], 0.0))
+    V(v.memset(T.dg[:, :], 0.0))
     wait("v", "p", p_pi)
-    V(v.tensor_scalar(T.p15[:, :], T.pi[:, :], 15, None, A.bitwise_and))
-    x = V(v.tensor_scalar(T.p96[:, :], T.pi[:, :], 96, None, A.bitwise_and))
+    V(v.tensor_scalar(T.p96[:, :], T.pi[:, :], 96, None, A.bitwise_and))
+    x = V(v.tensor_scalar(T.p15[:, :], T.pi[:, :], 15, None, A.bitwise_and))
     wait("v", "v", x)
+    wait("v", "p", p_eye)
+    V(v.tensor_copy(T.dg[:, 3:515:4], T.eye[:, :]))
     V(v.tensor_copy(T.icol[:, :], T.p15[:, :]))
-    V(v.tensor_scalar(T.ic74[:, :], T.p15[:, :], float(M), None, A.mult))
-    x = V(v.tensor_scalar(T.pcol[:, :], T.p96[:, :], 5.0, None, A.mult))
+    V(v.tensor_scalar(T.ncol[:, :], T.p96[:, :], -STEP / 32.0, None, A.mult))
+    V(v.tensor_scalar(T.jcol[:, :], T.p15[:, :], float(HELD + K), None, A.add))
+    for t in range(N):
+        x = V(v.memset(T.pcol[32 * t:32 * t + 32, :], float(STEP * t + CAP * order.index(t))))
+    wait("s", "v", x)
+    wait("s", "p", p_b16)
+    Sc(sc.activation(T.vals[:, :], T.jj[:, :], ID, bias=T.pcol[:, 0:1]))
+    Sc(sc.activation(T.jw[:, :], T.b16[:, :], ID, bias=T.jcol[:, 0:1]))
+    for h in range(2):
+        s_con = Sc(sc.activation(T.zt[:, 256 * h:256 * h + 256], T.ones[:, 0:256], COPY, scale=0.0))
     wait("v", "v", x)
-    wait("v", "p", p_b16)
-    V(v.tensor_scalar(T.kk[:, :], T.kb[:, :], T.ic74[:, 0:1], None, A.add))
-    V(v.tensor_scalar(T.vals[:, :], T.jj[:, :], T.pcol[:, 0:1], None, A.add))
-    V(v.tensor_scalar(T.jw[:, :], T.b16[:, :], T.icol[:, 0:1], float(K), A.add, A.add))
-    x = V(v.tensor_scalar(T.ff[:, :], T.b16[:, 0:30], T.icol[:, 0:1], None, A.add))
-    wait("v", "v", x)
-    V(v.tensor_scalar(T.fq[:, :], T.ff[:, :], 1.0 / 30.0, -29.0 / 60.0, A.mult, A.add))
-    x = V(v.tensor_scalar(T.fb[:, :], T.ff[:, :], 16.0, None, A.mult))
-    wait("v", "v", x)
-    x = V(v.tensor_scalar(T.fa[:, :], T.fq[:, :], -479.0, None, A.mult))
-    wait("v", "v", x)
-    x = V(v.tensor_tensor(T.fc[:, :], T.fa[:, :], T.fb[:, :], A.add))
-    wait("v", "v", x)
-    V(v.tensor_copy(T.pmo[:, :], T.fc[:, :]))
-    V(v.quantize_mx(T.land[:, K:K + 128], T.lands[:, K:K + 128], T.zt[:, :]))
+    for b in range(4):
+        V(v.quantize_mx(T.ec[:, 128 * b:128 * b + 128], T.es[:, 128 * b:128 * b + 128], T.dg[:, 3 - b:515 - b]))
+    wait("v", "p", p_kb)
+    V(v.tensor_scalar(T.kk[:, :], T.kb[:, :], T.icol[:, 0:1], None, A.add))
+    wait("v", "s", s_dm)
+    V(v.tensor_scalar(T.dm[:, 3:515:4], T.eye[:, :], -0.125, None, A.mult))
 
     wait("v", "ltc", 128)
-    V(v.tensor_scalar(T.la[:, :], T.tcl[:, :], 15, None, A.bitwise_and))
-    V(v.tensor_scalar(T.lb[:, :], T.tcl[:, :], 4, None, A.arith_shift_right))
-    x = V(v.tensor_scalar(T.ln[:, :], T.tcl[:, :], 0.0, None, A.is_lt))
+    tl = T.tcl
+    if order != [0, 1, 2, 3]:
+        tl = T.tcr
+        for k, w, n in runs(order):
+            V(v.tensor_copy(T.tcr[:, 32 + k:32 + k + n], T.tcl[:, 32 + w:32 + w + n]))
+    wait("v", "lx", 48)
+    x = V(v.transpose(tl[:, 0:32], T.xl[:, :]))
     wait("v", "v", x)
-    V(v.tensor_scalar(T.la2[:, :], T.la[:, :], float(M), None, A.mult))
-    x = V(v.tensor_tensor(T.ln2[:, :], T.ln[:, :], T.kk[:, :], A.mult))
-    wait("v", "v", x)
-    x = V(v.tensor_tensor(T.ls[:, :], T.la2[:, :], T.lb[:, :], A.add))
-    wait("v", "v", x)
-    x = V(v.tensor_tensor(T.lp[:, :], T.ls[:, :], T.ln2[:, :], A.add))
-    wait("v", "v", x)
-    for t in range(N):
-        x = V(v.tensor_copy(T.lto[32 * t:32 * t + 32, :], T.lp[32 * t:32 * t + 32, 10 * t:10 * t + 10]))
-    wait("v", "v", x)
-    v_scat = V(v.tensor_copy(T.win[:, :].indirect(T.lto[:, :]), T.vals[:, :]))
-    V(v.tensor_copy(T.poso[:, :], T.lp[:, 0:30]))
-    v_wo = V(v.tensor_copy(T.wo[:, :], T.tcl[:, :]))
-    wait("v", "lsn", 128)
-    V(v.tensor_copy(T.sno[:, :], T.snl[:, :]))
+    v_wo = V(v.tensor_copy(T.wo[:, :], tl[:, 32:72]))
+    V(v.tensor_scalar(T.la[:, :], tl[:, :], 15, None, A.bitwise_and))
+    V(v.tensor_scalar(T.lb[:, :], tl[:, :], 4, None, A.arith_shift_right))
+    V(v.tensor_scalar(T.ln[:, :], tl[:, 32:72], 0.0, None, A.is_lt))
 
     for h in range(2):
         wait("v", "lgr%d" % h, 16)
-        v_gq = V(v.quantize_mx(T.gq[:, 256 * h:256 * h + 256], T.gqs[:, 256 * h:256 * h + 256], T.grt[:, 1024 * h:1024 * h + 1024]))
-    wait("v", "v", v_gq)
-    wait("s", "v", v_gq)
-    runs = [(a, b) for a, b in ((0, 10 * rank), (10 * rank + 10, 40)) if b > a]
+        V(v.quantize_mx(T.gq[:, 256 * h:256 * h + 256], T.gqs[:, 256 * h:256 * h + 256], T.grt[:, 1024 * h:1024 * h + 1024]))
+    wait("v", "lsn", 128)
+    v_sno = V(v.tensor_copy(T.sno[:, :], T.snl[:, :]))
+    wait("v", "v", v_sno)
+    wait("s", "v", v_sno)
     at = 0
-    for a, b in runs:
+    for a, b in ((0, 10 * rank), (10 * rank + 10, 40)):
         n = 16 * (b - a)
-        v_snd = V(v.tensor_copy(u32(T.snd[:, at:at + n]), u32(T.gq[:, :]).indirect(T.sno[:, a:b])))
-        s_snd = Sc(sc.activation(T.snds[:, at:at + n], T.gqs[:, :].indirect(T.sno[:, a:b]), COPY))
+        if n:
+            v_snd = V(v.tensor_copy(u32(T.snd[:, at:at + n]), u32(T.gq[:, :]).indirect(T.sno[:, a:b])))
+            s_snd = Sc(sc.activation(T.snds[:, at:at + n], T.gqs[:, :].indirect(T.sno[:, a:b]), COPY))
         at += n
-    own = slice(CAP * rank, CAP * rank + CAP)
-    V(v.tensor_copy(u32(T.land[:, own]), u32(T.gq[:, :]).indirect(T.sno[:, 10 * rank:10 * rank + 10])))
-    s_own = Sc(sc.activation(T.lands[:, own], T.gqs[:, :].indirect(T.sno[:, 10 * rank:10 * rank + 10]), COPY))
 
     others = [q for q in range(N) if q != rank]
     sent = 0
@@ -179,95 +202,115 @@ def rank_program(g, core, T, topo):
         for k, o in enumerate(others):
             rid, pid, _ = topo.addr(cores[o])
             e = engines(core, cores[o], cores, topo)
-            src, to = T[buf][:, CAP * k:CAP * k + CAP], T[dst][:, own]
+            place = CAP * items(o).index(rank)
+            src, to = T[buf][:, CAP * k:CAP * k + CAP], T[dst][:, place:place + CAP]
             if buf == "snd":
                 src, to = u8(src), u8(to)
             transfers.append(RemoteDMATransfer(dst_ids=[DstId(rid=rid, pnc=pid)], dma_engine_mask=bits(e), remote_sem=T.sem.arr, src=src, dst=to))
             sent += len(e)
         wait("g", q, need)
         g.remote_dma_fused(transfers, local_sem=T.sem.loc)
+    g.sem_inc(T.sem.go)
     arrive = sum(len(f(cores[o], core, cores, topo)) for o in others for f in (code_engines, scale_engines))
 
-    wait("v", "p", p_dg)
-    V(v.tensor_scalar(T.dm[:, :], T.dg[:, :], -0.125, None, A.mult))
-    for b in range(4):
-        x = V(v.quantize_mx(T.ec[:, 128 * b:128 * b + 128], T.es[:, 128 * b:128 * b + 128], T.dg[:, 3 - b:515 - b]))
+    v_wi, s_wi = {}, {}
+
+    def pick_w(h, a, b):
+        v_wi[h] = V(v.tensor_copy(u32(T.wi[:, 16 * a:16 * b]), u32(T.wsrc[:, :]).indirect(T.wo[:, a:b])))
+        s_wi[h] = Sc(sc.activation(T.wis[:, 16 * a:16 * b], T.wsrcs[:, :].indirect(T.wo[:, a:b]), COPY))
+
     wait("v", "lw", 32)
     wait("s", "lw", 32)
-    wait("s", "v", v_wo)
-    v_wi = V(v.tensor_copy(u32(T.wi[:, :]), u32(T.wsrc[:, :]).indirect(T.wo[:, :])))
-    s_wi = Sc(sc.activation(T.wis[:, :], T.wsrcs[:, :].indirect(T.wo[:, :]), COPY))
+    pick_w(0, 0, 30)
+    x = V(v.tensor_scalar(T.la2[:, :], T.la[:, :], float(M), None, A.mult))
+    V(v.tensor_tensor(T.ln2[:, :], T.ln[:, :], T.kk[:, :], A.mult))
     wait("v", "v", x)
+    x = V(v.tensor_tensor(T.ls[:, :], T.la2[:, :], T.lb[:, :], A.add))
+    wait("v", "v", x)
+    x = V(v.tensor_tensor(T.lp[:, :], T.ls[:, 32:72], T.ln2[:, :], A.add))
+    wait("v", "v", x)
+    for t in range(N):
+        k = order.index(t)
+        x = V(v.tensor_copy(T.lto[32 * t:32 * t + 32, :], T.lp[32 * t:32 * t + 32, 10 * k:10 * k + 10]))
+    wait("v", "v", x)
+    wait("v", "s", s_con)
+    v_scat = V(v.tensor_copy(T.win[:, :].indirect(T.lto[:, :]), T.vals[:, :]))
+    v_poso = V(v.tensor_copy(T.poso[:, :], T.ls[:, 0:32]))
+    pick_w(1, 30, 40)
+    wait("s", "v", v_poso)
+    s_rn = Sc(sc.activation(T.rn[:, :], T.win[:, :].indirect(T.poso[:, :]), ID, bias=T.ncol[:, 0:1]))
     for b in range(4):
-        v_m = V(v.quantize_mx(T.mc[:, 128 * b:128 * b + 128], T.ms[:, 128 * b:128 * b + 128], T.dm[:, 3 - b:515 - b]))
+        V(v.quantize_mx(T.mc[:, 128 * b:128 * b + 128], T.ms[:, 128 * b:128 * b + 128], T.dm[:, 3 - b:515 - b]))
+    v_own = V(v.tensor_copy(u32(T.land[:, H0:K]), u32(T.gq[:, :]).indirect(T.sno[:, 10 * rank:10 * rank + 10])))
+    s_own = Sc(sc.activation(T.lands[:, H0:K], T.gqs[:, :].indirect(T.sno[:, 10 * rank:10 * rank + 10]), COPY))
+    V(v.quantize_mx(T.land[:, K:K + 128], T.lands[:, K:K + 128], T.zt[:, :]))
 
-    def product(const, b, half, mov, movs, first, last):
+    t_done = {}
+
+    def product(const, half, n, mov, movs, first, last):
         c, s_ = (T.ec, T.es) if const == "e" else (T.mc, T.ms)
-        n = H0 if half == 0 else CAP
-        bank = 512 * (4 * half + b)
-        return te.matmul_mx(T.ps[:, bank:bank + n], c[:, 128 * b:128 * b + 128], s_[:, 128 * b:128 * b + 128], mov, movs, first, last)
+        for b in range(4):
+            bank = 512 * (4 * half + b)
+            t_done[(b, half)] = done("t", te.matmul_mx(T.ps[:, bank:bank + n], c[:, 128 * b:128 * b + 128], s_[:, 128 * b:128 * b + 128],
+                                                       mov, movs, first, last))
 
-    wait("t", "v", v_wi)
-    wait("t", "s", s_wi)
-    for b in range(4):
-        product("e", b, 0, T.wi[:, 0:H0], T.wis[:, 0:H0], True, False)
-    for b in range(4):
-        product("e", b, 1, T.wi[:, H0:K], T.wis[:, H0:K], True, False)
-
-    x = Sc(sc.activation(T.rn[:, :], T.win[:, :].indirect(T.poso[:, :]), COPY))
-    wait("s", "s", x)
-    s_rp = Sc(sc.activation(T.rp[:, :], T.rn[:, :].indirect(T.pmo[:, :]), COPY))
+    for h, (a, b) in enumerate(((0, H0), (H0, K))):
+        wait("t", "v", v_wi[h])
+        wait("t", "s", s_wi[h])
+        product("e", h, b - a, T.wi[:, a:b], T.wis[:, a:b], True, False)
+    wait("t", "v", v_own)
+    wait("t", "s", s_own)
+    product("m", 1, CAP, T.land[:, H0:K], T.lands[:, H0:K], False, rank == 3)
 
     wait("y", "v", v_scat)
     for t in range(N):
-        sy.dma_start(T.fw[:, M * t:M * t + M], T.win[32 * t:32 * t + 8, :]).then_inc(T.sem.xf, 16)
-    wait("y", "s", s_rp)
+        sy.dma_start(T.fw[:, M * t:M * t + M], T.win[32 * t:32 * t + 8, 0:C]).then_inc(T.sem.xf, 16)
+    wait("y", "s", s_rn)
     for k, t in enumerate((3, 2, 1)):
-        sy.dma_start(T.rw[:, 30 * k:30 * k + 30], T.rp[32 * t:32 * t + 8, :]).then_inc(T.sem.xr, 16)
+        sy.dma_start(T.rw[:, 32 * k:32 * k + 32], T.rn[32 * t:32 * t + 8, :]).then_inc(T.sem.xr, 16)
+    wait("y", "go", 1)
     sy.dma_start(u8(T.tab[:, K:K + C]), T.wc[:, :]).then_inc(T.sem.ltab, 16)
     sy.dma_start(T.tabs[:, K:K + C], T.ws[:, :]).then_inc(T.sem.ltab, 16)
 
     wait("v", "xf", 64)
     x = V(v.tensor_tensor(T.f1[:, :], T.fw[:, 0:2 * M], T.fw[:, 2 * M:4 * M], A.min))
     wait("v", "v", x)
-    x = V(v.tensor_tensor(T.f2[:, :], T.f1[:, 0:64], T.f1[:, M:M + 64], A.min))
+    x = V(v.tensor_tensor(T.f2[:, :], T.f1[:, 0:M], T.f1[:, M:2 * M], A.min))
     wait("v", "v", x)
     x = V(v.tensor_tensor(T.f3[:, :], T.f2[:, :], T.jw[:, :], A.min))
     wait("v", "v", x)
-    V(v.tensor_copy(T.fino[:, :], T.f3[:, :]))
+    x = V(v.tensor_scalar(T.f4[:, :], T.f3[:, :], STEP - 1, None, A.bitwise_and))
+    wait("v", "v", x)
+    V(v.tensor_copy(T.fino[:, :], T.f4[:, :]))
     wait("v", "xr", 48)
-    x = V(v.tensor_tensor(T.rw[:, 0:20], T.rw[:, 0:20], T.rw[:, 30:50], A.min))
+    x = V(v.tensor_tensor(T.rw[:, 0:20], T.rw[:, 0:20], T.rw[:, 32:52], A.min))
     wait("v", "v", x)
-    x = V(v.tensor_tensor(T.rw[:, 0:10], T.rw[:, 0:10], T.rw[:, 60:70], A.min))
+    x = V(v.tensor_tensor(T.rw[:, 0:10], T.rw[:, 0:10], T.rw[:, 64:74], A.min))
     wait("v", "v", x)
-    v_paro = V(v.tensor_scalar(T.paro[:, :], T.rw[:, 0:30], float(K), None, A.min))
+    for k, w, n in runs(par):
+        v_paro = V(v.tensor_scalar(T.paro[:, k:k + n], T.rw[:, w:w + n], float(K), None, A.min))
 
-    wait("v", "arr", arrive)
-    wait("s", "arr", arrive)
-    wait("t", "arr", arrive)
+    for q in "vst":
+        wait(q, "arr", arrive)
     wait("v", "v", v_paro)
     wait("s", "v", v_paro)
     wait("s", "s", s_own)
     v_par = V(v.tensor_copy(u32(T.par[:, :]), u32(T.land[:, :]).indirect(T.paro[:, :])))
     s_par = Sc(sc.activation(T.pars[:, :], T.lands[:, :].indirect(T.paro[:, :]), COPY))
 
-    wait("t", "v", v_m)
-    wait("t", "s", s_own)
-    for b in range(4):
-        product("m", b, 0, T.land[:, 0:H0], T.lands[:, 0:H0], False, False)
+    product("m", 0, H0, T.land[:, 0:H0], T.lands[:, 0:H0], False, False)
     wait("t", "v", v_par)
     wait("t", "s", s_par)
-    t_done = {}
-    for b in range(4):
-        t_done[(b, 0)] = done("t", product("m", b, 0, T.par[:, :], T.pars[:, :], False, True))
-    for b in range(4):
-        t_done[(b, 1)] = done("t", product("m", b, 1, T.land[:, H0:K], T.lands[:, H0:K], False, True))
+    n = H0 if rank == 3 else 2 * CAP
+    product("m", 0, n, T.par[:, 0:n], T.pars[:, 0:n], False, True)
+    if rank != 3:
+        product("m", 1, CAP, T.par[:, n:H0], T.pars[:, n:H0], False, True)
 
-    x = V(v.tensor_scalar(T.c1[0:32, :], T.fw[0:32, :], float(K), None, A.is_lt))
+    x = V(v.tensor_scalar(T.c1[0:32, :], T.fw[0:32, :], float(HELD), None, A.is_lt))
     wait("v", "v", x)
     x = V(v.tensor_tensor(T.c2[0:32, :], T.c1[0:32, 0:2 * M], T.c1[0:32, 2 * M:4 * M], A.add))
     wait("v", "v", x)
-    x = V(v.tensor_tensor(T.c3[0:32, :], T.c2[0:32, 0:64], T.c2[0:32, M:M + 64], A.add))
+    x = V(v.tensor_tensor(T.c3[0:32, :], T.c2[0:32, 0:M], T.c2[0:32, M:2 * M], A.add))
     wait("v", "v", x)
     v_up = V(v.transpose(T.c4[0:32, :], T.c3[0:32, :]))
     wait("y", "v", v_up)
@@ -275,44 +318,46 @@ def rank_program(g, core, T, topo):
         sy.dma_start(T.up[0:1, 512 * b:512 * b + 512], T.c4[0:32, 32 * b:32 * b + 16]).then_inc(T.sem.stored, 16)
         count["stored"] += 16
 
-    last = {}
-
     def cast(q, b, half):
         lo, n = (0, H0) if half == 0 else (H0, CAP)
         wait(q, "t", t_done[(b, half)])
         bank = 512 * (4 * half + b)
         out, src = T.nw[:, 4 * lo + b:4 * (lo + n):4], T.ps[:, bank:bank + n]
-        if q == "v":
-            last["v"] = V(v.tensor_copy(out, src))
-        else:
-            last["s"] = Sc(sc.activation(out, src, COPY))
+        return V(v.tensor_copy(out, src)) if q == "v" else Sc(sc.activation(out, src, COPY))
 
+    def own_slots():
+        for b in range(4):
+            x = cast("s", b, 1)
+        wait("v", "s", x)
+        return V(v.quantize_mx(T.tab[:, H0:K], T.tabs[:, H0:K], T.nw[:, 4 * H0:4 * K]))
+
+    if rank == 3:
+        own_slots()
     cast("s", 0, 0)
     cast("v", 1, 0)
-    cast("s", 2, 0)
-    cast("v", 3, 0)
-    wait("v", "v", last["v"])
-    wait("v", "s", last["s"])
-    V(v.quantize_mx(T.tab[:, 0:H0], T.tabs[:, 0:H0], T.nw[:, 0:4 * H0]))
-    for b in range(4):
-        cast("s", b, 1)
-    wait("v", "s", last["s"])
-    v_new = V(v.quantize_mx(T.tab[:, H0:K], T.tabs[:, H0:K], T.nw[:, 4 * H0:4 * K]))
+    y = cast("s", 2, 0)
+    x = cast("v", 3, 0)
+    wait("v", "v", x)
+    wait("v", "s", y)
+    v_new = V(v.quantize_mx(T.tab[:, 0:H0], T.tabs[:, 0:H0], T.nw[:, 0:4 * H0]))
+    if rank != 3:
+        v_new = own_slots()
 
     wait("v", "ltab", 32)
     wait("s", "ltab", 32)
     wait("v", "v", v_new)
     wait("s", "v", v_new)
-    for h in range(2):
-        lst = T.fino[:, 32 * h:32 * h + 32]
-        x = V(v.tensor_copy(u32(T.fin[:, 512 * h:512 * h + 512]), u32(T.tab[:, :]).indirect(lst)))
-        s_fin = Sc(sc.activation(T.fins[:, 512 * h:512 * h + 512], T.tabs[:, :].indirect(lst), COPY))
+    for a, b in ((0, 24), (24, 48), (48, 64)):
+        lst = T.fino[:, a:b]
+        x = V(v.tensor_copy(u32(T.fin[:, 16 * a:16 * b]), u32(T.tab[:, :]).indirect(lst)))
+        s_fin = Sc(sc.activation(T.fins[:, 16 * a:16 * b], T.tabs[:, :].indirect(lst), COPY))
         wait("y", "v", x)
-        sy.dma_start(T.oc[:, 2048 * h:2048 * h + 2048], u8(T.fin[:, 512 * h:512 * h + 512])).then_inc(T.sem.stored, 16)
+        sy.dma_start(T.oc[:, 64 * a:64 * b], u8(T.fin[:, 16 * a:16 * b])).then_inc(T.sem.stored, 16)
         count["stored"] += 16
     wait("s", "s", s_fin)
+    wait("y", "s", s_fin)
     for k in range(4):
-        sc.dma_start(T.osc[4 * k:4 * k + 4, :], T.fins[32 * k:32 * k + 4, :]).then_inc(T.sem.stored, 16)
+        (sc if k < 2 else sy).dma_start(T.osc[4 * k:4 * k + 4, :], T.fins[32 * k:32 * k + 4, :]).then_inc(T.sem.stored, 16)
         count["stored"] += 16
     wait("y", "stored", count["stored"])
 

@@ -5,10 +5,8 @@ C, S, CAP, N = 1024, 512, 160, 4
 K = N * CAP
 H0 = 3 * CAP
 M = C // 16
-WIN = C + CAP
-STEP = 2048
-HELD = 4 * STEP
-NONE = 2.0 * HELD
+HELD = K + CAP
+DUMP = 288
 X4 = "float8_e4m3fn_x4"
 
 
@@ -17,45 +15,25 @@ def _sb(dtype, **widths):
 
 
 SCRATCH = {
-    **_sb("bfloat16", ones=296, eye=128, dg=516, dm=516, zt=512, grt=4 * S, nw=4 * K),
-    **_sb(X4, ec=512, mc=512, gq=S, snd=H0, land=K + 128, wsrc=C, wi=K, par=H0, tab=K + C, fin=C),
-    **_sb("uint8", es=512, ms=512, gqs=S, snds=H0, lands=K + 128, wsrcs=C, wis=K, pars=H0, tabs=K + C, fins=C),
-    **_sb("int32", pi=1, p15=1, p96=1, kb=40, kk=40, tcl=72, tcr=72, la=72, lb=72, la2=72, ls=72, ln=40, ln2=40, lp=40,
-          xl=32, snl=40, f3=64, f4=64),
-    **_sb("float32", icol=1, jcol=1, pcol=1, ncol=1, jj=CAP, vals=CAP, b16=64, jw=64, win=WIN, rn=512, rw=96,
-          fw=4 * M, f1=2 * M, f2=64, c1=4 * M, c2=2 * M, c3=64, c4=64),
+    **_sb("bfloat16", ones=256, eye=128, dg=516, dm=516, zt=512, grt=4 * S, nw=4 * K),
+    **_sb(X4, ec=512, mc=512, gq=S, snd=H0, land=K + 128, wsrc=C, wi=K, par=H0, tab=HELD + C, fin=C),
+    **_sb("uint8", es=512, ms=512, gqs=S, snds=H0, lands=K + 128, wsrcs=C, wis=K, pars=H0, tabs=HELD + C, fins=C),
+    **_sb("int32", tl=42, hi=42, tcl=40, xl=32, snl=40),
+    **_sb("float32", kb=10, ke=10, jj=CAP, pcol=1, rcol=1, vals=CAP, win=DUMP + C, h2=42, u=42, lp=10, rn=512, rw=96,
+          rm=20, fw=4 * M, f1=2 * M, f2=M, c1=4 * M, c2=2 * M, c3=64, c4=64, c5=64),
     **_sb("uint16", sno=40, wo=40, lto=10, poso=32, paro=30, fino=64),
     "ps": ("psum", [128, 4096], "float32"),
 }
-SEMAPHORES = ["v", "s", "t", "p", "ltc", "lx", "lsn", "lgr0", "lgr1", "lw", "ltab", "xf", "xr", "stored", "arr", "loc", "go"]
-
-
-def partners(rank):
-    return [s for s in range(3) if s != rank] + [rank] if rank != 3 else [0, 1, 2]
+SEMAPHORES = ["v", "s", "t", "p", "ltl", "ltc", "lx", "lsn", "lgr0", "lgr1", "lw", "ltab", "xf", "xr", "stored", "arr", "loc", "go"]
 
 
 def items(rank):
     return [s for s in range(N) if s != rank] + [rank]
 
 
-def code_engines(src, dst, cores, topo):
+def engines(src, dst, topo, scales):
     e = topo.engines(src, dst)
-    even, odd = e[0::2], e[1::2]
-    if topo.die(src) == topo.die(dst):
-        return odd
-    far = [c for c in cores if topo.die(c) != topo.die(src)]
-    h = len(even) // 2
-    return even[:h] if far.index(dst) == 0 else even[h:]
-
-
-def scale_engines(src, dst, cores, topo):
-    e = topo.engines(src, dst)
-    even, odd = e[0::2], e[1::2]
-    if topo.die(src) == topo.die(dst):
-        return even[:len(even) // 2]
-    far = [c for c in cores if topo.die(c) != topo.die(src)]
-    h = len(odd) // 2
-    return odd[:h] if far.index(dst) == 0 else odd[h:]
+    return e[(topo.die(src) == topo.die(dst)) != scales::2]
 
 
 def bits(e):
@@ -65,18 +43,29 @@ def bits(e):
     return m
 
 
+def runs(where):
+    k, r = 0, []
+    while k < len(where):
+        n = 1
+        while k + n < len(where) and where[k + n] == where[k] + n:
+            n += 1
+        r.append((k, where[k], n))
+        k += n
+    return r
+
+
 def rank_program(g, core, T, topo):
     rank = T.rank_of(core)
     if rank is None:
         return
     cores = list(T.cores)
-    A = AluOpType
-    COPY, ID = ActivationFunctionType.Copy, ActivationFunctionType.Identity
+    A, AF = AluOpType, ActivationFunctionType
     v, sc, te, sy = g.vector, g.scalar, g.tensor, g.sync
     queue = {"g": g, "v": v, "s": sc, "t": te, "y": sy}
     count = {"v": 0, "s": 0, "t": 0, "p": 0, "stored": 0}
     seen = {}
-    order, par = items(rank), partners(rank)
+    order = items(rank)
+    others = order[:3]
 
     def wait(q, sem, val):
         if seen.get((q, sem), 0) < val:
@@ -103,256 +92,247 @@ def rank_program(g, core, T, topo):
     def u32(ap):
         return ap.bitcast(dt.uint32)
 
-    def runs(where):
-        k, r = 0, []
-        while k < len(where):
-            n = 1
-            while k + n < len(where) and where[k + n] == where[k] + n:
-                n += 1
-            r.append((10 * k, 10 * where[k], 10 * n))
-            k += n
-        return r
+    def pick(out, at, src, lst, a, b, only="vs"):
+        n = 16 * (b - a)
+        o = T[lst][:, a:b]
+        x = y = None
+        if "v" in only:
+            x = V(v.tensor_copy(u32(T[out][:, at:at + n]), u32(T[src][:, :]).indirect(o)))
+        if "s" in only:
+            y = Sc(sc.activation(T[out + "s"][:, at:at + n], T[src + "s"][:, :].indirect(o), AF.Copy))
+        return x, y
 
     v_xl = V(v.memset(T.xl[:, :], 0))
     v_ones = V(v.memset(T.ones[:, :], 1.0))
-    for q, lo in ((sy, 0), (sc, 4)):
+
+    def load_gr(q, h):
+        q.dma_start(T.grt[:, 1024 * h:1024 * h + 1024], T.gr[:, 1024 * h:1024 * h + 1024]).then_inc(T.sem["lgr%d" % h], 16)
+
+    def load_tl(q, lo):
         for u in range(lo, lo + 4):
-            q.dma_start(T.tcl[16 * u:16 * u + 16, 32:72], T.tc[:, :]).then_inc(T.sem.ltc, 16)
+            q.dma_start(T.tl[16 * u:16 * u + 16, 32:42], T.tc[:, 10 * (u // 2):10 * (u // 2) + 10]).then_inc(T.sem.ltl, 16)
+
+    def load_sn(q, lo):
+        for u in range(lo, lo + 4):
+            q.dma_start(T.snl[16 * u:16 * u + 16, :], T.sn[:, :]).then_inc(T.sem.lsn, 16)
+
+    load_gr(sc, 0)
+    load_tl(sc, 0)
+    load_sn(sc, 0)
+    load_tl(sy, 4)
     wait("y", "v", v_xl)
     for t in (1, 2, 3):
         sy.dma_start(T.xl[32 * t:32 * t + 32, 0:16], T.tc[:, 0:32]).then_inc(T.sem.lx, 16)
-    for h, q in ((0, sc), (1, sy)):
-        q.dma_start(T.grt[:, 1024 * h:1024 * h + 1024], T.gr[:, 1024 * h:1024 * h + 1024]).then_inc(T.sem["lgr%d" % h], 16)
-        for u in range(4 * h, 4 * h + 4):
-            q.dma_start(T.snl[16 * u:16 * u + 16, :], T.sn[:, :]).then_inc(T.sem.lsn, 16)
+    load_gr(sy, 1)
+    load_sn(sy, 4)
+    for u in range(8):
+        sy.dma_start(T.tcl[16 * u:16 * u + 16, :], T.tc[:, :]).then_inc(T.sem.ltc, 16)
     sy.dma_start(u8(T.wsrc[:, :]), T.wc[:, :]).then_inc(T.sem.lw, 16)
-    sc.dma_start(T.wsrcs[:, :], T.ws[:, :]).then_inc(T.sem.lw, 16)
+    sy.dma_start(T.wsrcs[:, :], T.ws[:, :]).then_inc(T.sem.lw, 16)
 
-    p_pi = P(g.iota(T.pi[:, :], [[0, 1]], 0, 1))
     wait("g", "v", v_ones)
     p_eye = P(g.affine_select(T.eye[:, :], T.ones[:, 0:128], [[-1, 128]], A.is_equal, 0.0, 0, 1))
-    p_kb = P(g.iota(T.kb[:, :], [[0, 4], [16, 10]], C - (15 * M - 1), 0))
-    P(g.iota(T.jj[:, :], [[1, CAP]], 0, 0, allow_small_or_imprecise_dtypes=True))
-    p_b16 = P(g.iota(T.b16[:, :], [[16, 64]], 0, 0, allow_small_or_imprecise_dtypes=True))
-    wait("s", "v", v_ones)
-    for h in range(2):
-        s_dm = Sc(sc.activation(T.dm[:, 258 * h:258 * h + 258], T.ones[:, 0:258], COPY, scale=0.0))
-    for h in range(4):
-        Sc(sc.activation(T.win[:, 296 * h:296 * h + 296], T.ones[:, :], COPY, scale=NONE))
+    p_win = P(g.iota(T.win[:, DUMP:DUMP + C // 2], [[1, 8], [16, M]], HELD, 0, allow_small_or_imprecise_dtypes=True))
+    p_kb = P(g.iota(T.kb[:, :], [[16, 10]], -DUMP, 1, allow_small_or_imprecise_dtypes=True))
+    p_jj = P(g.iota(T.jj[:, :], [[1, CAP]], 0, 0, allow_small_or_imprecise_dtypes=True))
 
     V(v.memset(T.dg[:, :], 0.0))
-    wait("v", "p", p_pi)
-    V(v.tensor_scalar(T.p96[:, :], T.pi[:, :], 96, None, A.bitwise_and))
-    x = V(v.tensor_scalar(T.p15[:, :], T.pi[:, :], 15, None, A.bitwise_and))
-    wait("v", "v", x)
-    wait("v", "p", p_eye)
-    V(v.tensor_copy(T.dg[:, 3:515:4], T.eye[:, :]))
-    V(v.tensor_copy(T.icol[:, :], T.p15[:, :]))
-    V(v.tensor_scalar(T.ncol[:, :], T.p96[:, :], -STEP / 32.0, None, A.mult))
-    V(v.tensor_scalar(T.jcol[:, :], T.p15[:, :], float(HELD + K), None, A.add))
     for t in range(N):
-        x = V(v.memset(T.pcol[32 * t:32 * t + 32, :], float(STEP * t + CAP * order.index(t))))
-    wait("s", "v", x)
-    wait("s", "p", p_b16)
-    Sc(sc.activation(T.vals[:, :], T.jj[:, :], ID, bias=T.pcol[:, 0:1]))
-    Sc(sc.activation(T.jw[:, :], T.b16[:, :], ID, bias=T.jcol[:, 0:1]))
-    for h in range(2):
-        s_con = Sc(sc.activation(T.zt[:, 256 * h:256 * h + 256], T.ones[:, 0:256], COPY, scale=0.0))
-    wait("v", "v", x)
-    for b in range(4):
-        V(v.quantize_mx(T.ec[:, 128 * b:128 * b + 128], T.es[:, 128 * b:128 * b + 128], T.dg[:, 3 - b:515 - b]))
-    wait("v", "p", p_kb)
-    V(v.tensor_scalar(T.kk[:, :], T.kb[:, :], T.icol[:, 0:1], None, A.add))
-    wait("v", "s", s_dm)
-    V(v.tensor_scalar(T.dm[:, 3:515:4], T.eye[:, :], -0.125, None, A.mult))
+        V(v.memset(T.pcol[32 * t:32 * t + 32, :], float(CAP * t)))
+    place = [K + CAP * t - CAP * order.index(t) for t in range(N)]
+    place[0] = place[1]
+    for t, n in ((0, 2), (2, 1), (3, 1)) if place[2] != place[3] else ((0, 2), (2, 2)):
+        v_rcol = V(v.memset(T.rcol[32 * t:32 * t + 32 * n, :], float(place[t])))
+    wait("v", "p", p_eye)
+    wait("v", "v", v_rcol)
+    v_dg = V(v.tensor_copy(T.dg[:, 3:515:4], T.eye[:, :]))
 
-    wait("v", "ltc", 128)
-    tl = T.tcl
-    if order != [0, 1, 2, 3]:
-        tl = T.tcr
-        for k, w, n in runs(order):
-            V(v.tensor_copy(T.tcr[:, 32 + k:32 + k + n], T.tcl[:, 32 + w:32 + w + n]))
+    wait("s", "v", v_ones)
+    for h in range(2):
+        s_zt = Sc(sc.activation(T.zt[:, 256 * h:256 * h + 256], T.ones[:, :], AF.Copy, scale=0.0))
+    wait("s", "v", v_dg)
+    s_dm = Sc(sc.activation(T.dm[:, :], T.dg[:, :], AF.Copy, scale=-0.125))
+    wait("s", "p", p_win)
+    Sc(sc.activation(T.win[:, DUMP + C // 2:DUMP + C], T.win[:, DUMP:DUMP + C // 2], AF.Identity, bias=8.0))
+    wait("s", "p", p_kb)
+    Sc(sc.activation(T.ke[:, :], T.kb[:, :], AF.Copy, scale=1.0 / M))
+    wait("s", "p", p_jj)
+    s_con = Sc(sc.activation(T.vals[:, :], T.jj[:, :], AF.Identity, bias=T.pcol[:, 0:1]))
+
+    def constants(code, scale, tile):
+        for b in range(4):
+            V(v.quantize_mx(T[code][:, 128 * b:128 * b + 128], T[scale][:, 128 * b:128 * b + 128], T[tile][:, 3 - b:515 - b]))
+
+    wait("v", "v", v_dg)
+    constants("ec", "es", "dg")
+
     wait("v", "lx", 48)
-    x = V(v.transpose(tl[:, 0:32], T.xl[:, :]))
+    x = V(v.transpose(T.tl[:, 0:32], T.xl[:, :]))
+    wait("v", "ltl", 128)
     wait("v", "v", x)
-    v_wo = V(v.tensor_copy(T.wo[:, :], tl[:, 32:72]))
-    V(v.tensor_scalar(T.la[:, :], tl[:, :], 15, None, A.bitwise_and))
-    V(v.tensor_scalar(T.lb[:, :], tl[:, :], 4, None, A.arith_shift_right))
-    V(v.tensor_scalar(T.ln[:, :], tl[:, 32:72], 0.0, None, A.is_lt))
+    x = V(v.tensor_scalar(T.hi[:, :], T.tl[:, :], 4, None, A.logical_shift_right))
+    wait("v", "v", x)
+    v_h2 = V(v.tensor_scalar(T.h2[:, :], T.hi[:, :], -(16.0 * M - 1) / M, None, A.mult))
 
     for h in range(2):
         wait("v", "lgr%d" % h, 16)
         V(v.quantize_mx(T.gq[:, 256 * h:256 * h + 256], T.gqs[:, 256 * h:256 * h + 256], T.grt[:, 1024 * h:1024 * h + 1024]))
     wait("v", "lsn", 128)
     v_sno = V(v.tensor_copy(T.sno[:, :], T.snl[:, :]))
+    wait("v", "v", v_h2)
+    v_u = V(v.tensor_tensor(T.u[:, :], T.tl[:, :], T.h2[:, :], A.add))
     wait("v", "v", v_sno)
     wait("s", "v", v_sno)
-    at = 0
-    for a, b in ((0, 10 * rank), (10 * rank + 10, 40)):
-        n = 16 * (b - a)
-        if n:
-            v_snd = V(v.tensor_copy(u32(T.snd[:, at:at + n]), u32(T.gq[:, :]).indirect(T.sno[:, a:b])))
-            s_snd = Sc(sc.activation(T.snds[:, at:at + n], T.gqs[:, :].indirect(T.sno[:, a:b]), COPY))
-        at += n
-
-    others = [q for q in range(N) if q != rank]
-    sent = 0
-    for buf, dst, engines, q, need in (("snd", "land", code_engines, "v", v_snd), ("snds", "lands", scale_engines, "s", s_snd)):
-        transfers = []
-        for k, o in enumerate(others):
-            rid, pid, _ = topo.addr(cores[o])
-            e = engines(core, cores[o], cores, topo)
-            place = CAP * items(o).index(rank)
-            src, to = T[buf][:, CAP * k:CAP * k + CAP], T[dst][:, place:place + CAP]
-            if buf == "snd":
-                src, to = u8(src), u8(to)
-            transfers.append(RemoteDMATransfer(dst_ids=[DstId(rid=rid, pnc=pid)], dma_engine_mask=bits(e), remote_sem=T.sem.arr, src=src, dst=to))
-            sent += len(e)
-        wait("g", q, need)
-        g.remote_dma_fused(transfers, local_sem=T.sem.loc)
+    first = N - 1 - rank
+    for dests in ([first], [o for o in others if o != first]):
+        base = 0 if dests[0] == first else CAP
+        for k, w, n in runs(dests):
+            need = pick("snd", base + CAP * k, "gq", "sno", 10 * w, 10 * w + 10 * n)
+        for buf, to, scales in (("snd", "land", False), ("snds", "lands", True)):
+            transfers = []
+            for k, o in enumerate(dests):
+                rid, pid, _ = topo.addr(cores[o])
+                at, there = base + CAP * k, CAP * items(o).index(rank)
+                src, dst = T[buf][:, at:at + CAP], T[to][:, there:there + CAP]
+                if not scales:
+                    src, dst = u8(src), u8(dst)
+                transfers.append(RemoteDMATransfer(dst_ids=[DstId(rid=rid, pnc=pid)], dma_engine_mask=bits(engines(core, cores[o], topo, scales)),
+                                                   remote_sem=T.sem.arr, src=src, dst=dst))
+            wait("g", "s" if scales else "v", need[scales])
+            g.remote_dma_fused(transfers, local_sem=T.sem.loc)
     g.sem_inc(T.sem.go)
-    arrive = sum(len(f(cores[o], core, cores, topo)) for o in others for f in (code_engines, scale_engines))
+    sent = sum(len(engines(core, cores[o], topo, f)) for o in others for f in (False, True))
+    arrive = sum(len(engines(cores[o], core, topo, f)) for o in others for f in (False, True))
 
-    v_wi, s_wi = {}, {}
-
-    def pick_w(h, a, b):
-        v_wi[h] = V(v.tensor_copy(u32(T.wi[:, 16 * a:16 * b]), u32(T.wsrc[:, :]).indirect(T.wo[:, a:b])))
-        s_wi[h] = Sc(sc.activation(T.wis[:, 16 * a:16 * b], T.wsrcs[:, :].indirect(T.wo[:, a:b]), COPY))
-
-    wait("v", "lw", 32)
-    wait("s", "lw", 32)
-    pick_w(0, 0, 30)
-    x = V(v.tensor_scalar(T.la2[:, :], T.la[:, :], float(M), None, A.mult))
-    V(v.tensor_tensor(T.ln2[:, :], T.ln[:, :], T.kk[:, :], A.mult))
-    wait("v", "v", x)
-    x = V(v.tensor_tensor(T.ls[:, :], T.la2[:, :], T.lb[:, :], A.add))
-    wait("v", "v", x)
-    x = V(v.tensor_tensor(T.lp[:, :], T.ls[:, 32:72], T.ln2[:, :], A.add))
-    wait("v", "v", x)
-    for t in range(N):
-        k = order.index(t)
-        x = V(v.tensor_copy(T.lto[32 * t:32 * t + 32, :], T.lp[32 * t:32 * t + 32, 10 * k:10 * k + 10]))
-    wait("v", "v", x)
+    wait("v", "v", v_u)
     wait("v", "s", s_con)
+    x = V(v.tensor_tensor(T.lp[:, :], T.u[:, 32:42], T.ke[:, :], A.max))
+    V(v.tensor_scalar(T.poso[:, :], T.u[:, 0:32], float(M), 0.0, A.mult, A.max))
+    wait("v", "v", x)
+    x = V(v.tensor_scalar(T.lto[:, :], T.lp[:, :], float(M), float(DUMP), A.mult, A.add))
+    wait("v", "ltc", 128)
+    v_wo = V(v.tensor_copy(T.wo[:, :], T.tcl[:, :]))
+    wait("v", "v", x)
     v_scat = V(v.tensor_copy(T.win[:, :].indirect(T.lto[:, :]), T.vals[:, :]))
-    v_poso = V(v.tensor_copy(T.poso[:, :], T.ls[:, 0:32]))
-    pick_w(1, 30, 40)
-    wait("s", "v", v_poso)
-    s_rn = Sc(sc.activation(T.rn[:, :], T.win[:, :].indirect(T.poso[:, :]), ID, bias=T.ncol[:, 0:1]))
-    for b in range(4):
-        V(v.quantize_mx(T.mc[:, 128 * b:128 * b + 128], T.ms[:, 128 * b:128 * b + 128], T.dm[:, 3 - b:515 - b]))
-    v_own = V(v.tensor_copy(u32(T.land[:, H0:K]), u32(T.gq[:, :]).indirect(T.sno[:, 10 * rank:10 * rank + 10])))
-    s_own = Sc(sc.activation(T.lands[:, H0:K], T.gqs[:, :].indirect(T.sno[:, 10 * rank:10 * rank + 10]), COPY))
-    V(v.quantize_mx(T.land[:, K:K + 128], T.lands[:, K:K + 128], T.zt[:, :]))
-
-    t_done = {}
-
-    def product(const, half, n, mov, movs, first, last):
-        c, s_ = (T.ec, T.es) if const == "e" else (T.mc, T.ms)
-        for b in range(4):
-            bank = 512 * (4 * half + b)
-            t_done[(b, half)] = done("t", te.matmul_mx(T.ps[:, bank:bank + n], c[:, 128 * b:128 * b + 128], s_[:, 128 * b:128 * b + 128],
-                                                       mov, movs, first, last))
-
-    for h, (a, b) in enumerate(((0, H0), (H0, K))):
-        wait("t", "v", v_wi[h])
-        wait("t", "s", s_wi[h])
-        product("e", h, b - a, T.wi[:, a:b], T.wis[:, a:b], True, False)
-    wait("t", "v", v_own)
-    wait("t", "s", s_own)
-    product("m", 1, CAP, T.land[:, H0:K], T.lands[:, H0:K], False, rank == 3)
-
+    wait("s", "v", v_wo)
+    wait("s", "lw", 32)
+    for k, w, n in runs(others):
+        s_others = pick("wi", CAP * k, "wsrc", "wo", 10 * w, 10 * w + 10 * n, "s")[1]
+    wait("s", "v", v_scat)
+    s_rn = Sc(sc.activation(T.rn[:, :], T.win[:, DUMP:DUMP + C].indirect(T.poso[:, :]), AF.Relu, bias=T.rcol[:, 0:1], scale=-1.0))
     wait("y", "v", v_scat)
     for t in range(N):
-        sy.dma_start(T.fw[:, M * t:M * t + M], T.win[32 * t:32 * t + 8, 0:C]).then_inc(T.sem.xf, 16)
+        sy.dma_start(T.fw[:, M * t:M * t + M], T.win[32 * t:32 * t + 8, DUMP:DUMP + C]).then_inc(T.sem.xf, 16)
     wait("y", "s", s_rn)
     for k, t in enumerate((3, 2, 1)):
         sy.dma_start(T.rw[:, 32 * k:32 * k + 32], T.rn[32 * t:32 * t + 8, :]).then_inc(T.sem.xr, 16)
     wait("y", "go", 1)
-    sy.dma_start(u8(T.tab[:, K:K + C]), T.wc[:, :]).then_inc(T.sem.ltab, 16)
-    sy.dma_start(T.tabs[:, K:K + C], T.ws[:, :]).then_inc(T.sem.ltab, 16)
+    sy.dma_start(u8(T.tab[:, HELD:HELD + C]), T.wc[:, :]).then_inc(T.sem.ltab, 16)
+    sy.dma_start(T.tabs[:, HELD:HELD + C], T.ws[:, :]).then_inc(T.sem.ltab, 16)
 
-    wait("v", "xf", 64)
-    x = V(v.tensor_tensor(T.f1[:, :], T.fw[:, 0:2 * M], T.fw[:, 2 * M:4 * M], A.min))
-    wait("v", "v", x)
-    x = V(v.tensor_tensor(T.f2[:, :], T.f1[:, 0:M], T.f1[:, M:2 * M], A.min))
-    wait("v", "v", x)
-    x = V(v.tensor_tensor(T.f3[:, :], T.f2[:, :], T.jw[:, :], A.min))
-    wait("v", "v", x)
-    x = V(v.tensor_scalar(T.f4[:, :], T.f3[:, :], STEP - 1, None, A.bitwise_and))
-    wait("v", "v", x)
-    V(v.tensor_copy(T.fino[:, :], T.f4[:, :]))
+    wait("v", "lw", 32)
+    wait("v", "v", v_wo)
+    for k, w, n in runs(others):
+        v_others = pick("wi", CAP * k, "wsrc", "wo", 10 * w, 10 * w + 10 * n, "v")[0]
+    w_own = pick("wi", H0, "wsrc", "wo", 10 * rank, 10 * rank + 10)
+    wait("v", "s", s_dm)
+    constants("mc", "ms", "dm")
+    own = pick("land", H0, "gq", "sno", 10 * rank, 10 * rank + 10)
+    wait("v", "s", s_zt)
+    V(v.quantize_mx(T.land[:, K:K + 128], T.lands[:, K:K + 128], T.zt[:, :]))
+
+    t_done = {}
+
+    def product(const, half, n, mov, at, need, start, last):
+        wait("t", "v", need[0])
+        wait("t", "s", need[1])
+        for b in range(4):
+            bank = 512 * (4 * half + b)
+            t_done[(b, half)] = done("t", te.matmul_mx(T.ps[:, bank:bank + n], T[const + "c"][:, 128 * b:128 * b + 128], T[const + "s"][:, 128 * b:128 * b + 128],
+                                                       T[mov][:, at:at + n], T[mov + "s"][:, at:at + n], start, last))
+
+    product("e", 0, H0, "wi", 0, (v_others, s_others), True, False)
+    product("e", 1, CAP, "wi", H0, w_own, True, False)
+    product("m", 1, CAP, "land", H0, own, False, rank == 3)
+
     wait("v", "xr", 48)
-    x = V(v.tensor_tensor(T.rw[:, 0:20], T.rw[:, 0:20], T.rw[:, 32:52], A.min))
+    x = V(v.tensor_tensor(T.rm[:, 0:20], T.rw[:, 0:20], T.rw[:, 32:52], A.max))
+    V(v.tensor_scalar(T.paro[:, 20:30], T.rw[:, 20:30], -1.0, float(K), A.mult, A.add))
     wait("v", "v", x)
-    x = V(v.tensor_tensor(T.rw[:, 0:10], T.rw[:, 0:10], T.rw[:, 64:74], A.min))
+    x = V(v.tensor_tensor(T.rm[:, 0:10], T.rm[:, 0:10], T.rw[:, 64:74], A.max))
     wait("v", "v", x)
-    for k, w, n in runs(par):
-        v_paro = V(v.tensor_scalar(T.paro[:, k:k + n], T.rw[:, w:w + n], float(K), None, A.min))
+    v_paro = V(v.tensor_scalar(T.paro[:, 0:20], T.rm[:, :], -1.0, float(K), A.mult, A.add))
+    wait("s", "xf", 64)
+    s_c1 = Sc(sc.activation(T.c1[0:32, :], T.fw[0:32, :], AF.Sign, bias=0.5 - HELD))
 
     for q in "vst":
         wait(q, "arr", arrive)
     wait("v", "v", v_paro)
     wait("s", "v", v_paro)
-    wait("s", "s", s_own)
-    v_par = V(v.tensor_copy(u32(T.par[:, :]), u32(T.land[:, :]).indirect(T.paro[:, :])))
-    s_par = Sc(sc.activation(T.pars[:, :], T.lands[:, :].indirect(T.paro[:, :]), COPY))
-
-    product("m", 0, H0, T.land[:, 0:H0], T.lands[:, 0:H0], False, False)
-    wait("t", "v", v_par)
-    wait("t", "s", s_par)
-    n = H0 if rank == 3 else 2 * CAP
-    product("m", 0, n, T.par[:, 0:n], T.pars[:, 0:n], False, True)
+    wait("s", "s", own[1])
+    with_partner = [s for s in others if s != N - 1]
     if rank != 3:
-        product("m", 1, CAP, T.par[:, n:H0], T.pars[:, n:H0], False, True)
+        p_own = pick("par", 2 * CAP, "land", "paro", 10 * rank, 10 * rank + 10)
+    for k, w, n in runs(with_partner):
+        p_others = pick("par", CAP * k, "land", "paro", 10 * w, 10 * w + 10 * n)
 
-    x = V(v.tensor_scalar(T.c1[0:32, :], T.fw[0:32, :], float(HELD), None, A.is_lt))
+    product("m", 0, H0, "land", 0, own, False, False)
+    if rank != 3:
+        product("m", 1, CAP, "par", 2 * CAP, p_own, False, True)
+    product("m", 0, CAP * len(with_partner), "par", 0, p_others, False, True)
+
+    wait("v", "xf", 64)
+    x = V(v.tensor_tensor(T.f1[:, :], T.fw[:, 0:2 * M], T.fw[:, 2 * M:4 * M], A.min))
+    wait("v", "s", s_c1)
+    y = V(v.tensor_tensor(T.c2[0:32, :], T.c1[0:32, 0:2 * M], T.c1[0:32, 2 * M:4 * M], A.add))
     wait("v", "v", x)
-    x = V(v.tensor_tensor(T.c2[0:32, :], T.c1[0:32, 0:2 * M], T.c1[0:32, 2 * M:4 * M], A.add))
+    x = V(v.tensor_tensor(T.f2[:, :], T.f1[:, 0:M], T.f1[:, M:2 * M], A.min))
+    wait("v", "v", y)
+    v_c3 = V(v.tensor_tensor(T.c3[0:32, :], T.c2[0:32, 0:M], T.c2[0:32, M:2 * M], A.add))
     wait("v", "v", x)
-    x = V(v.tensor_tensor(T.c3[0:32, :], T.c2[0:32, 0:M], T.c2[0:32, M:2 * M], A.add))
-    wait("v", "v", x)
-    v_up = V(v.transpose(T.c4[0:32, :], T.c3[0:32, :]))
-    wait("y", "v", v_up)
-    for b in range(2):
-        sy.dma_start(T.up[0:1, 512 * b:512 * b + 512], T.c4[0:32, 32 * b:32 * b + 16]).then_inc(T.sem.stored, 16)
-        count["stored"] += 16
+    V(v.tensor_copy(T.fino[:, :], T.f2[:, :]))
 
     def cast(q, b, half):
         lo, n = (0, H0) if half == 0 else (H0, CAP)
         wait(q, "t", t_done[(b, half)])
         bank = 512 * (4 * half + b)
         out, src = T.nw[:, 4 * lo + b:4 * (lo + n):4], T.ps[:, bank:bank + n]
-        return V(v.tensor_copy(out, src)) if q == "v" else Sc(sc.activation(out, src, COPY))
+        return V(v.tensor_copy(out, src)) if q == "v" else Sc(sc.activation(out, src, AF.Copy))
 
-    def own_slots():
-        for b in range(4):
-            x = cast("s", b, 1)
-        wait("v", "s", x)
-        return V(v.quantize_mx(T.tab[:, H0:K], T.tabs[:, H0:K], T.nw[:, 4 * H0:4 * K]))
+    def quantise(x, y, blocks):
+        wait("v", "v", x)
+        wait("v", "s", y)
+        for k, w, n in runs([order[b] for b in blocks]):
+            a, at, n = CAP * (blocks[0] + k), CAP * w, CAP * n
+            z = V(v.quantize_mx(T.tab[:, at:at + n], T.tabs[:, at:at + n], T.nw[:, 4 * a:4 * (a + n)]))
+        return z
 
-    if rank == 3:
-        own_slots()
+    cast("s", 0, 1)
+    y = cast("s", 2, 1)
+    cast("v", 1, 1)
+    x = cast("v", 3, 1)
     cast("s", 0, 0)
+    quantise(x, y, [3])
     cast("v", 1, 0)
     y = cast("s", 2, 0)
     x = cast("v", 3, 0)
-    wait("v", "v", x)
-    wait("v", "s", y)
-    v_new = V(v.quantize_mx(T.tab[:, 0:H0], T.tabs[:, 0:H0], T.nw[:, 0:4 * H0]))
-    if rank != 3:
-        v_new = own_slots()
+    wait("s", "v", v_c3)
+    s_c4 = Sc(sc.activation(T.c4[0:32, :], T.c3[0:32, :], AF.Identity, bias=2.0, scale=-0.5))
+    v_new = quantise(x, y, [0, 1, 2])
 
     wait("v", "ltab", 32)
     wait("s", "ltab", 32)
     wait("v", "v", v_new)
     wait("s", "v", v_new)
     for a, b in ((0, 24), (24, 48), (48, 64)):
-        lst = T.fino[:, a:b]
-        x = V(v.tensor_copy(u32(T.fin[:, 16 * a:16 * b]), u32(T.tab[:, :]).indirect(lst)))
-        s_fin = Sc(sc.activation(T.fins[:, 16 * a:16 * b], T.tabs[:, :].indirect(lst), COPY))
+        x, s_fin = pick("fin", 16 * a, "tab", "fino", a, b)
         wait("y", "v", x)
         sy.dma_start(T.oc[:, 64 * a:64 * b], u8(T.fin[:, 16 * a:16 * b])).then_inc(T.sem.stored, 16)
+        count["stored"] += 16
+    wait("v", "s", s_c4)
+    wait("y", "v", V(v.transpose(T.c5[0:32, :], T.c4[0:32, :])))
+    for b in range(2):
+        sy.dma_start(T.up[0:1, 512 * b:512 * b + 512], T.c5[0:32, 32 * b:32 * b + 16]).then_inc(T.sem.stored, 16)
         count["stored"] += 16
     wait("s", "s", s_fin)
     wait("y", "s", s_fin)

from concourse.bass import DstId, RemoteDMATransfer
from concourse.mybir import dt, AluOpType, ActivationFunctionType

C, S, CAP, N = 1024, 512, 160, 4
K = N * CAP
H0 = 3 * CAP
M = C // 16
HELD = K + CAP
DUMP = 288
X4 = "float8_e4m3fn_x4"


def _sb(dtype, **widths):
    return {name: ("sbuf", [128, n], dtype) for name, n in widths.items()}


SCRATCH = {
    **_sb("bfloat16", ones=256, eye=128, dg=516, dm=516, zt=512, grt=4 * S, nw=4 * K),
    **_sb(X4, ec=512, mc=512, gq=S, snd=H0, land=K + 128, wsrc=C, wi=K, par=H0, tab=HELD + C, fin=C),
    **_sb("uint8", es=512, ms=512, gqs=S, snds=H0, lands=K + 128, wsrcs=C, wis=K, pars=H0, tabs=HELD + C, fins=C),
    **_sb("int32", tl=42, hi=42, tcl=40, xl=32, snl=40),
    **_sb("float32", kb=10, ke=10, jj=CAP, pcol=1, rcol=1, vals=CAP, win=DUMP + C, h2=42, u=42, lp=10, rn=512, rw=96,
          rm=20, fw=4 * M, f1=2 * M, f2=M, c1=4 * M, c2=2 * M, c3=64, c4=64, c5=64),
    **_sb("uint16", sno=40, wo=40, lto=10, poso=32, paro=30, fino=64),
    "ps": ("psum", [128, 4096], "float32"),
}
SEMAPHORES = ["v", "s", "t", "p", "ltl", "ltc", "lx", "lsn", "lgr0", "lgr1", "lw", "ltab", "xf", "xr", "stored", "arr", "loc", "go"]


def items(rank):
    return [s for s in range(N) if s != rank] + [rank]


def engines(src, dst, topo, scales):
    e = topo.engines(src, dst)
    return e[(topo.die(src) == topo.die(dst)) != scales::2]


def bits(e):
    m = 0
    for k in e:
        m |= 1 << k
    return m


def runs(where):
    k, r = 0, []
    while k < len(where):
        n = 1
        while k + n < len(where) and where[k + n] == where[k] + n:
            n += 1
        r.append((k, where[k], n))
        k += n
    return r


def rank_program(g, core, T, topo):
    rank = T.rank_of(core)
    if rank is None:
        return
    cores = list(T.cores)
    A, AF = AluOpType, ActivationFunctionType
    v, sc, te, sy = g.vector, g.scalar, g.tensor, g.sync
    queue = {"g": g, "v": v, "s": sc, "t": te, "y": sy}
    count = {"v": 0, "s": 0, "t": 0, "p": 0, "stored": 0}
    seen = {}
    order = items(rank)
    others = order[:3]

    def wait(q, sem, val):
        if seen.get((q, sem), 0) < val:
            queue[q].wait_ge(T.sem[sem], val)
            seen[(q, sem)] = val

    def done(sem, ins):
        ins.then_inc(T.sem[sem], 1)
        count[sem] += 1
        return count[sem]

    def V(ins):
        return done("v", ins)

    def Sc(ins):
        return done("s", ins)

    def P(ins):
        return done("p", ins)

    def u8(ap):
        return ap.bitcast(dt.uint8)

    def u32(ap):
        return ap.bitcast(dt.uint32)

    def pick(out, at, src, lst, a, b, only="vs"):
        n = 16 * (b - a)
        o = T[lst][:, a:b]
        x = y = None
        if "v" in only:
            x = V(v.tensor_copy(u32(T[out][:, at:at + n]), u32(T[src][:, :]).indirect(o)))
        if "s" in only:
            y = Sc(sc.activation(T[out + "s"][:, at:at + n], T[src + "s"][:, :].indirect(o), AF.Copy))
        return x, y

    v_xl = V(v.memset(T.xl[:, :], 0))
    v_ones = V(v.memset(T.ones[:, :], 1.0))

    def load_gr(q, h):
        q.dma_start(T.grt[:, 1024 * h:1024 * h + 1024], T.gr[:, 1024 * h:1024 * h + 1024]).then_inc(T.sem["lgr%d" % h], 16)

    def load_tl(q, lo):
        for u in range(lo, lo + 4):
            q.dma_start(T.tl[16 * u:16 * u + 16, 32:42], T.tc[:, 10 * (u // 2):10 * (u // 2) + 10]).then_inc(T.sem.ltl, 16)

    def load_sn(q, lo):
        for u in range(lo, lo + 4):
            q.dma_start(T.snl[16 * u:16 * u + 16, :], T.sn[:, :]).then_inc(T.sem.lsn, 16)

    load_gr(sc, 0)
    load_tl(sc, 0)
    load_sn(sc, 0)
    load_tl(sy, 4)
    wait("y", "v", v_xl)
    for t in (1, 2, 3):
        sy.dma_start(T.xl[32 * t:32 * t + 32, 0:16], T.tc[:, 0:32]).then_inc(T.sem.lx, 16)
    load_gr(sy, 1)
    load_sn(sy, 4)
    for u in range(8):
        sy.dma_start(T.tcl[16 * u:16 * u + 16, :], T.tc[:, :]).then_inc(T.sem.ltc, 16)
    sy.dma_start(u8(T.wsrc[:, :]), T.wc[:, :]).then_inc(T.sem.lw, 16)
    sy.dma_start(T.wsrcs[:, :], T.ws[:, :]).then_inc(T.sem.lw, 16)

    wait("g", "v", v_ones)
    p_eye = P(g.affine_select(T.eye[:, :], T.ones[:, 0:128], [[-1, 128]], A.is_equal, 0.0, 0, 1))
    p_win = P(g.iota(T.win[:, DUMP:DUMP + C // 2], [[1, 8], [16, M]], HELD, 0, allow_small_or_imprecise_dtypes=True))
    p_kb = P(g.iota(T.kb[:, :], [[16, 10]], -DUMP, 1, allow_small_or_imprecise_dtypes=True))
    p_jj = P(g.iota(T.jj[:, :], [[1, CAP]], 0, 0, allow_small_or_imprecise_dtypes=True))

    V(v.memset(T.dg[:, :], 0.0))
    for t in range(N):
        V(v.memset(T.pcol[32 * t:32 * t + 32, :], float(CAP * t)))
    place = [K + CAP * t - CAP * order.index(t) for t in range(N)]
    place[0] = place[1]
    for t, n in ((0, 2), (2, 1), (3, 1)) if place[2] != place[3] else ((0, 2), (2, 2)):
        v_rcol = V(v.memset(T.rcol[32 * t:32 * t + 32 * n, :], float(place[t])))
    wait("v", "p", p_eye)
    wait("v", "v", v_rcol)
    v_dg = V(v.tensor_copy(T.dg[:, 3:515:4], T.eye[:, :]))

    wait("s", "v", v_ones)
    for h in range(2):
        s_zt = Sc(sc.activation(T.zt[:, 256 * h:256 * h + 256], T.ones[:, :], AF.Copy, scale=0.0))
    wait("s", "v", v_dg)
    s_dm = Sc(sc.activation(T.dm[:, :], T.dg[:, :], AF.Copy, scale=-0.125))
    wait("s", "p", p_win)
    Sc(sc.activation(T.win[:, DUMP + C // 2:DUMP + C], T.win[:, DUMP:DUMP + C // 2], AF.Identity, bias=8.0))
    wait("s", "p", p_kb)
    Sc(sc.activation(T.ke[:, :], T.kb[:, :], AF.Copy, scale=1.0 / M))
    wait("s", "p", p_jj)
    s_con = Sc(sc.activation(T.vals[:, :], T.jj[:, :], AF.Identity, bias=T.pcol[:, 0:1]))

    def constants(code, scale, tile):
        for b in range(4):
            V(v.quantize_mx(T[code][:, 128 * b:128 * b + 128], T[scale][:, 128 * b:128 * b + 128], T[tile][:, 3 - b:515 - b]))

    wait("v", "v", v_dg)
    constants("ec", "es", "dg")

    wait("v", "lx", 48)
    x = V(v.transpose(T.tl[:, 0:32], T.xl[:, :]))
    wait("v", "ltl", 128)
    wait("v", "v", x)
    x = V(v.tensor_scalar(T.hi[:, :], T.tl[:, :], 4, None, A.logical_shift_right))
    wait("v", "v", x)
    v_h2 = V(v.tensor_scalar(T.h2[:, :], T.hi[:, :], -(16.0 * M - 1) / M, None, A.mult))

    for h in range(2):
        wait("v", "lgr%d" % h, 16)
        V(v.quantize_mx(T.gq[:, 256 * h:256 * h + 256], T.gqs[:, 256 * h:256 * h + 256], T.grt[:, 1024 * h:1024 * h + 1024]))
    wait("v", "lsn", 128)
    v_sno = V(v.tensor_copy(T.sno[:, :], T.snl[:, :]))
    wait("v", "v", v_h2)
    v_u = V(v.tensor_tensor(T.u[:, :], T.tl[:, :], T.h2[:, :], A.add))
    wait("v", "v", v_sno)
    wait("s", "v", v_sno)
    first = N - 1 - rank
    for dests in ([first], [o for o in others if o != first]):
        base = 0 if dests[0] == first else CAP
        for k, w, n in runs(dests):
            need = pick("snd", base + CAP * k, "gq", "sno", 10 * w, 10 * w + 10 * n)
        for buf, to, scales in (("snd", "land", False), ("snds", "lands", True)):
            transfers = []
            for k, o in enumerate(dests):
                rid, pid, _ = topo.addr(cores[o])
                at, there = base + CAP * k, CAP * items(o).index(rank)
                src, dst = T[buf][:, at:at + CAP], T[to][:, there:there + CAP]
                if not scales:
                    src, dst = u8(src), u8(dst)
                transfers.append(RemoteDMATransfer(dst_ids=[DstId(rid=rid, pnc=pid)], dma_engine_mask=bits(engines(core, cores[o], topo, scales)),
                                                   remote_sem=T.sem.arr, src=src, dst=dst))
            wait("g", "s" if scales else "v", need[scales])
            g.remote_dma_fused(transfers, local_sem=T.sem.loc)
    g.sem_inc(T.sem.go)
    sent = sum(len(engines(core, cores[o], topo, f)) for o in others for f in (False, True))
    arrive = sum(len(engines(cores[o], core, topo, f)) for o in others for f in (False, True))

    wait("v", "v", v_u)
    wait("v", "s", s_con)
    x = V(v.tensor_tensor(T.lp[:, :], T.u[:, 32:42], T.ke[:, :], A.max))
    V(v.tensor_scalar(T.poso[:, :], T.u[:, 0:32], float(M), 0.0, A.mult, A.max))
    wait("v", "v", x)
    x = V(v.tensor_scalar(T.lto[:, :], T.lp[:, :], float(M), float(DUMP), A.mult, A.add))
    wait("v", "ltc", 128)
    v_wo = V(v.tensor_copy(T.wo[:, :], T.tcl[:, :]))
    wait("v", "v", x)
    v_scat = V(v.tensor_copy(T.win[:, :].indirect(T.lto[:, :]), T.vals[:, :]))
    wait("s", "v", v_wo)
    wait("s", "lw", 32)
    for k, w, n in runs(others):
        s_others = pick("wi", CAP * k, "wsrc", "wo", 10 * w, 10 * w + 10 * n, "s")[1]
    wait("s", "v", v_scat)
    s_rn = Sc(sc.activation(T.rn[:, :], T.win[:, DUMP:DUMP + C].indirect(T.poso[:, :]), AF.Relu, bias=T.rcol[:, 0:1], scale=-1.0))
    wait("y", "v", v_scat)
    for t in range(N):
        sy.dma_start(T.fw[:, M * t:M * t + M], T.win[32 * t:32 * t + 8, DUMP:DUMP + C]).then_inc(T.sem.xf, 16)
    wait("y", "s", s_rn)
    for k, t in enumerate((3, 2, 1)):
        sy.dma_start(T.rw[:, 32 * k:32 * k + 32], T.rn[32 * t:32 * t + 8, :]).then_inc(T.sem.xr, 16)
    wait("y", "go", 1)
    sy.dma_start(u8(T.tab[:, HELD:HELD + C]), T.wc[:, :]).then_inc(T.sem.ltab, 16)
    sy.dma_start(T.tabs[:, HELD:HELD + C], T.ws[:, :]).then_inc(T.sem.ltab, 16)

    wait("v", "lw", 32)
    wait("v", "v", v_wo)
    for k, w, n in runs(others):
        v_others = pick("wi", CAP * k, "wsrc", "wo", 10 * w, 10 * w + 10 * n, "v")[0]
    w_own = pick("wi", H0, "wsrc", "wo", 10 * rank, 10 * rank + 10)
    wait("v", "s", s_dm)
    constants("mc", "ms", "dm")
    own = pick("land", H0, "gq", "sno", 10 * rank, 10 * rank + 10)
    wait("v", "s", s_zt)
    V(v.quantize_mx(T.land[:, K:K + 128], T.lands[:, K:K + 128], T.zt[:, :]))

    t_done = {}

    def product(const, half, n, mov, at, need, start, last):
        wait("t", "v", need[0])
        wait("t", "s", need[1])
        for b in range(4):
            bank = 512 * (4 * half + b)
            t_done[(b, half)] = done("t", te.matmul_mx(T.ps[:, bank:bank + n], T[const + "c"][:, 128 * b:128 * b + 128], T[const + "s"][:, 128 * b:128 * b + 128],
                                                       T[mov][:, at:at + n], T[mov + "s"][:, at:at + n], start, last))

    product("e", 0, H0, "wi", 0, (v_others, s_others), True, False)
    product("e", 1, CAP, "wi", H0, w_own, True, False)
    product("m", 1, CAP, "land", H0, own, False, rank == 3)

    wait("v", "xr", 48)
    x = V(v.tensor_tensor(T.rm[:, 0:20], T.rw[:, 0:20], T.rw[:, 32:52], A.max))
    V(v.tensor_scalar(T.paro[:, 20:30], T.rw[:, 20:30], -1.0, float(K), A.mult, A.add))
    wait("v", "v", x)
    x = V(v.tensor_tensor(T.rm[:, 0:10], T.rm[:, 0:10], T.rw[:, 64:74], A.max))
    wait("v", "v", x)
    v_paro = V(v.tensor_scalar(T.paro[:, 0:20], T.rm[:, :], -1.0, float(K), A.mult, A.add))
    wait("s", "xf", 64)
    s_c1 = Sc(sc.activation(T.c1[0:32, :], T.fw[0:32, :], AF.Sign, bias=0.5 - HELD))

    for q in "vst":
        wait(q, "arr", arrive)
    wait("v", "v", v_paro)
    wait("s", "v", v_paro)
    wait("s", "s", own[1])
    with_partner = [s for s in others if s != N - 1]
    if rank != 3:
        p_own = pick("par", 2 * CAP, "land", "paro", 10 * rank, 10 * rank + 10)
    for k, w, n in runs(with_partner):
        p_others = pick("par", CAP * k, "land", "paro", 10 * w, 10 * w + 10 * n)

    product("m", 0, H0, "land", 0, own, False, False)
    if rank != 3:
        product("m", 1, CAP, "par", 2 * CAP, p_own, False, True)
    product("m", 0, CAP * len(with_partner), "par", 0, p_others, False, True)

    wait("v", "xf", 64)
    x = V(v.tensor_tensor(T.f1[:, :], T.fw[:, 0:2 * M], T.fw[:, 2 * M:4 * M], A.min))
    wait("v", "s", s_c1)
    y = V(v.tensor_tensor(T.c2[0:32, :], T.c1[0:32, 0:2 * M], T.c1[0:32, 2 * M:4 * M], A.add))
    wait("v", "v", x)
    x = V(v.tensor_tensor(T.f2[:, :], T.f1[:, 0:M], T.f1[:, M:2 * M], A.min))
    wait("v", "v", y)
    v_c3 = V(v.tensor_tensor(T.c3[0:32, :], T.c2[0:32, 0:M], T.c2[0:32, M:2 * M], A.add))
    wait("v", "v", x)
    V(v.tensor_copy(T.fino[:, :], T.f2[:, :]))

    def cast(q, b, half):
        lo, n = (0, H0) if half == 0 else (H0, CAP)
        wait(q, "t", t_done[(b, half)])
        bank = 512 * (4 * half + b)
        out, src = T.nw[:, 4 * lo + b:4 * (lo + n):4], T.ps[:, bank:bank + n]
        return V(v.tensor_copy(out, src)) if q == "v" else Sc(sc.activation(out, src, AF.Copy))

    def quantise(x, y, blocks):
        wait("v", "v", x)
        wait("v", "s", y)
        for k, w, n in runs([order[b] for b in blocks]):
            a, at, n = CAP * (blocks[0] + k), CAP * w, CAP * n
            z = V(v.quantize_mx(T.tab[:, at:at + n], T.tabs[:, at:at + n], T.nw[:, 4 * a:4 * (a + n)]))
        return z

    cast("s", 0, 1)
    y = cast("s", 2, 1)
    cast("v", 1, 1)
    x = cast("v", 3, 1)
    cast("s", 0, 0)
    quantise(x, y, [3])
    cast("v", 1, 0)
    y = cast("s", 2, 0)
    x = cast("v", 3, 0)
    wait("s", "v", v_c3)
    s_c4 = Sc(sc.activation(T.c4[0:32, :], T.c3[0:32, :], AF.Identity, bias=2.0, scale=-0.5))
    v_new = quantise(x, y, [0, 1, 2])

    wait("v", "ltab", 32)
    wait("s", "ltab", 32)
    wait("v", "v", v_new)
    wait("s", "v", v_new)
    for a, b in ((0, 24), (24, 48), (48, 64)):
        x, s_fin = pick("fin", 16 * a, "tab", "fino", a, b)
        wait("y", "v", x)
        sy.dma_start(T.oc[:, 64 * a:64 * b], u8(T.fin[:, 16 * a:16 * b])).then_inc(T.sem.stored, 16)
        count["stored"] += 16
    wait("v", "s", s_c4)
    wait("y", "v", V(v.transpose(T.c5[0:32, :], T.c4[0:32, :])))
    for b in range(2):
        sy.dma_start(T.up[0:1, 512 * b:512 * b + 512], T.c5[0:32, 32 * b:32 * b + 16]).then_inc(T.sem.stored, 16)
        count["stored"] += 16
    wait("s", "s", s_fin)
    wait("y", "s", s_fin)
    for k in range(4):
        (sc if k < 2 else sy).dma_start(T.osc[4 * k:4 * k + 4, :], T.fins[32 * k:32 * k + 4, :]).then_inc(T.sem.stored, 16)
        count["stored"] += 16
    wait("y", "stored", count["stored"])

    wait("g", "loc", sent)
    for sem in ("v", "s", "t", "p"):
        wait("g", sem, count[sem])
